import numpy as np
import ml_dtypes


def mxq(x, axis, fmt="e4m3"):
    dtype, down = {"e4m3": (ml_dtypes.float8_e4m3fn, 7), "e5m2": (ml_dtypes.float8_e5m2, 14)}[fmt]
    v = np.moveaxis(np.asarray(x, np.float32).astype(ml_dtypes.bfloat16).astype(np.float64), axis, -1)
    blocks = v.reshape(v.shape[:-1] + (-1, 32))
    amax = np.abs(blocks).max(-1, keepdims=True)
    byte = np.maximum(np.where(amax > 0, np.frexp(amax)[1] - 1 + 127, 0) - down, 1)
    scale = np.exp2(byte - 127.0)
    codes = (blocks / scale).astype(np.float32).astype(dtype).astype(np.float64)
    return np.moveaxis((codes * scale).reshape(v.shape), -1, axis)


WIDE = False


def mx_kscale(k):
    if not WIDE:
        return np.ones(k)
    levels = np.array([10, -10, 5, -5, 0])
    if k % 512:
        return np.exp2(np.random.permutation(np.resize(levels, k // 32))).repeat(32)
    a = np.empty((k // 512, 16))
    for p in range(k // 512):
        a[p, :8] = np.random.permutation(np.resize(levels, 8))
        for g in range(8):
            far = levels[np.abs(levels - a[p, g]) >= 10]
            a[p, g + 8] = far[np.random.randint(len(far))]
    return np.exp2(a.ravel()).repeat(32)


def f64(x):
    return np.asarray(x).astype(np.float64)


def striped(idx):
    return np.tile(idx.reshape(-1, 16).T, (8, 1)).astype(np.uint16)


def unstriped(offs):
    return offs[:16].T.reshape(-1).astype(np.int64)


E2M1 = np.array([0.0, 0.5, 1.0, 1.5, 2.0, 3.0, 4.0, 6.0, -0.0, -0.5, -1.0, -1.5, -2.0, -3.0, -4.0, -6.0])


def pack_fp4(w):
    k, n = w.shape
    w = f64(np.asarray(w, np.float32).astype(ml_dtypes.bfloat16)).reshape(k // 32, 32, n)
    amax = np.abs(w).max(1)
    mant, ex = np.frexp(amax / 6.0)
    byte = np.clip(np.where(amax > 0, np.where(mant > 0.5, ex, ex - 1) + 127, 1), 1, 254)
    scaled = (w * np.exp2(127.0 - byte)[:, None, :]).reshape(k, n).astype(np.float32)
    c = np.ascontiguousarray(scaled.reshape(k // 512, 128, 4, n).transpose(0, 1, 3, 2)).astype(ml_dtypes.float4_e2m1fn).view(np.uint8) & 0xF
    words = (c[..., 0::2] | (c[..., 1::2] << 4)).reshape(k // 512, 128, 2 * n)
    return np.ascontiguousarray(words), np.ascontiguousarray(byte.astype(np.uint8).reshape(k // 512, 16, n))


def unpack_fp4(words, scales):
    g, _, n = scales.shape
    words = np.ascontiguousarray(words).reshape(g, 128, n, 2)
    nib = np.empty((g, 128, n, 4), np.uint8)
    nib[..., 0::2] = words & 0xF
    nib[..., 1::2] = words >> 4
    vals = E2M1[nib] * np.repeat(np.exp2(scales.astype(np.float64) - 127.0), 8, axis=1)[..., None]
    return vals.transpose(0, 1, 3, 2).reshape(g * 512, n)


K, T, S, N, U = 512, 2048, 1024, 128, 1024


def setup_inputs():
    n = np.random.standard_normal
    s = mx_kscale(K)[:, None]
    packed_w1 = pack_fp4(n((K, N)) / np.sqrt(K) / s)
    return {
        "xT": (n((K, T)) * s).astype(np.float32),
        "w1_words": packed_w1[0],
        "w1_scales": packed_w1[1],
        "gamma": np.random.uniform(0.5, 1.5, (N, U)).astype(np.float32),
        "beta": (0.5 * n((N, U))).astype(np.float32),
        "offs": striped(np.random.permutation(T)[:S]),
        "cls": striped(np.random.randint(0, U, S)),
    }


def reference(xT, w1_words, w1_scales, gamma, beta, offs, cls):
    xq = mxq(f64(xT)[:, unstriped(offs)], 0, "e4m3")
    y = unpack_fp4(w1_words, w1_scales).T @ xq
    g = f64(gamma)[:, unstriped(cls)]
    s = f64(beta)[:, unstriped(cls)]
    return y * g + s

@@ -1,0 +1,132 @@
+from contextlib import ExitStack
+
+import concourse.mybir as mybir
+
+K, T, S, N, U = 512, 2048, 1024, 128, 1024
+FLOPS = 2 * K * S * N + 2 * S * N
+
+F32 = mybir.dt.float32
+BF16 = mybir.dt.bfloat16
+I32 = mybir.dt.int32
+U32 = mybir.dt.uint32
+U16 = mybir.dt.uint16
+U8 = mybir.dt.uint8
+FP8X4 = mybir.dt.float8_e4m3fn_x4
+FP4X4 = mybir.dt.float4_e2m1fn_x4
+COPY = mybir.ActivationFunctionType.Copy
+MULT = mybir.AluOpType.mult
+ADD = mybir.AluOpType.add
+
+P = 128
+PACK = 4
+STRIPE = 16
+CHUNK = 256
+ROW2_WIDTHS = (1024, 1024)
+PAIR_WIDTHS = (1024, 640, 384)
+ROW3_WIDTHS = (512, 512, 512, 512)
+
+
+def spans(widths):
+    result = []
+    start = 0
+    for width in widths:
+        result.append(slice(start, start + width))
+        start = start + width
+    return result
+
+
+def tile_picked_cbn_none_e_kernel(tc, xT, w1_words, w1_scales, gamma, beta, offs, cls, out):
+    nc = tc.nc
+    chunks = S // CHUNK
+    x_rows = xT.rearrange("(p j) t -> p j t", j=PACK)
+
+    with ExitStack() as ctx:
+        keep = ctx.enter_context(tc.tile_pool(name="keep", bufs=1))
+        psum = ctx.enter_context(tc.psum_pool(name="psum", bufs=1))
+
+        offs_sb = keep.tile([P, S // STRIPE], U16, name="offs_sb")
+        cls_sb = keep.tile([P, S // STRIPE], U16, name="cls_sb")
+        gamma_sb = keep.tile([P, U], F32, name="gamma_sb")
+        beta_sb = keep.tile([P, U], F32, name="beta_sb")
+        row2_raw = [keep.tile([P, c.stop - c.start], F32, name=f"row2_raw{i}") for i, c in enumerate(spans(ROW2_WIDTHS))]
+        pair_raw = [keep.tile([P, 2, c.stop - c.start], F32, name=f"pair_raw{i}") for i, c in enumerate(spans(PAIR_WIDTHS))]
+        row3_raw = [keep.tile([P, c.stop - c.start], F32, name=f"row3_raw{i}") for i, c in enumerate(spans(ROW3_WIDTHS))]
+
+        nc.sync.dma_start(gamma_sb[:], gamma)
+        nc.sync.dma_start(cls_sb[:], cls)
+        nc.sync.dma_start(offs_sb[:], offs)
+        for raw, c in zip(row2_raw, spans(ROW2_WIDTHS)):
+            nc.sync.dma_start(raw[:], x_rows[:, 2, c])
+        for raw, c in zip(pair_raw, spans(PAIR_WIDTHS)):
+            nc.sync.dma_start(raw[:], x_rows[:, 0:2, c])
+        for raw, c in zip(row3_raw, spans(ROW3_WIDTHS)):
+            nc.sync.dma_start(raw[:], x_rows[:, 3, c])
+        nc.sync.dma_start(beta_sb[:], beta)
+
+        w_codes = keep.tile([P, 2 * N], U8, name="w_codes", align_bytes=64)
+        w_scales = keep.tile([P, N], U8, name="w_scales", align_bytes=64)
+        nc.gpsimd.memset(w_scales[:], 0)
+        nc.gpsimd.dma_start(w_codes[:].bitcast(I32), w1_words[0].bitcast(I32))
+        for quad in range(4):
+            nc.gpsimd.dma_start(
+                w_scales[32 * quad : 32 * quad + 4, :].bitcast(I32),
+                w1_scales[0, 4 * quad : 4 * quad + 4, :].bitcast(I32),
+            )
+
+        def entries(lst, first, count):
+            return lst[:, first // STRIPE : (first + count) // STRIPE]
+
+        gamma_picked = keep.tile([P, S], F32, name="gamma_picked")
+        for first in range(0, S, 512):
+            nc.vector.tensor_copy(gamma_picked[:, first : first + 512], gamma_sb[:].indirect(entries(cls_sb, first, 512)))
+
+        row2 = keep.tile([P, T], BF16, name="row2")
+        row3 = keep.tile([P, T], BF16, name="row3")
+        pair = keep.tile([P, T, 2], BF16, name="pair")
+        picked = [keep.tile([P, CHUNK, PACK], BF16, name=f"picked{i}", align_bytes=64) for i in range(chunks)]
+
+        for raw, c in zip(row2_raw, spans(ROW2_WIDTHS)):
+            nc.scalar.activation(row2[:, c], raw[:], COPY)
+        for i in range(chunks):
+            nc.scalar.activation(picked[i][:, :, 2], row2[:].indirect(entries(offs_sb, i * CHUNK, CHUNK)), COPY)
+
+        for raw, c in zip(pair_raw, spans(PAIR_WIDTHS)):
+            nc.vector.tensor_copy(pair[:, c, :], raw[:].rearrange("p j t -> p t j"))
+        pair_words = pair[:].rearrange("p t j -> p (t j)").bitcast(U32)
+        for i in range(chunks):
+            words = picked[i][:].rearrange("p s j -> p (s j)").bitcast(U32)
+            nc.vector.tensor_copy(words[:, 0 : 2 * CHUNK : 2], pair_words.indirect(entries(offs_sb, i * CHUNK, CHUNK)))
+
+        for raw, c in zip(row3_raw, spans(ROW3_WIDTHS)):
+            nc.scalar.activation(row3[:, c], raw[:], COPY)
+        for i in range(chunks):
+            nc.scalar.activation(picked[i][:, :, 3], row3[:].indirect(entries(offs_sb, i * CHUNK, CHUNK)), COPY)
+
+        def quantise_and_multiply(i):
+            codes = keep.tile([P, CHUNK], U32, name=f"codes{i}", tag=f"slot{i}", align_bytes=64)
+            scales = keep.tile([P, CHUNK], U8, name=f"scales{i}", align_bytes=64)
+            nc.vector.quantize_mx(out=codes[:].bitcast(FP8X4), scales=scales[:], in_=picked[i][:].rearrange("p s j -> p (s j)"))
+            acc = psum.tile([P, CHUNK], F32, name=f"acc{i}")
+            nc.tensor.matmul_mx(
+                out=acc[:],
+                lhsT=w_codes[:].bitcast(FP4X4),
+                lhsT_scale=w_scales[:],
+                rhs=codes[:].bitcast(FP8X4),
+                rhs_scale=scales[:],
+                start=True,
+                stop=True,
+            )
+            return acc
+
+        def scale(i, acc):
+            scaled = keep.tile([P, CHUNK], F32, name=f"scaled{i}", tag=f"slot{i + 2}", align_bytes=64)
+            nc.vector.tensor_tensor(scaled[:], acc[:], gamma_picked[:, i * CHUNK : (i + 1) * CHUNK], MULT)
+            return scaled
+
+        def shift_and_store(i, scaled):
+            result = keep.tile([P, CHUNK], F32, name=f"result{i}")
+            nc.vector.tensor_tensor(result[:], beta_sb[:].indirect(entries(cls_sb, i * CHUNK, CHUNK)), scaled[:], ADD)
+            nc.sync.dma_start(out[:, i * CHUNK : (i + 1) * CHUNK], result[:])
+
+        for i in range(chunks):
+            shift_and_store(i, scale(i, quantise_and_multiply(i)))

@@ -21,7 +21,7 @@ P = 128
 PACK = 4
 STRIPE = 16
 CHUNK = 256
-ROW2_WIDTHS = (1024, 1024)
+ROW2_WIDTHS = (2048,)
 PAIR_WIDTHS = (1024, 640, 384)
 ROW3_WIDTHS = (512, 512, 512, 512)
 
@@ -52,26 +52,26 @@ def tile_picked_cbn_none_e_kernel(tc, xT, w1_words, w1_scales, gamma, beta, offs
         pair_raw = [keep.tile([P, 2, c.stop - c.start], F32, name=f"pair_raw{i}") for i, c in enumerate(spans(PAIR_WIDTHS))]
         row3_raw = [keep.tile([P, c.stop - c.start], F32, name=f"row3_raw{i}") for i, c in enumerate(spans(ROW3_WIDTHS))]
 
+        w_codes = keep.tile([P, 2 * N], U8, name="w_codes", align_bytes=64)
+        w_scales = keep.tile([P, N], U8, name="w_scales", align_bytes=64)
+        nc.gpsimd.memset(w_scales[:], 0)
         nc.sync.dma_start(gamma_sb[:], gamma)
         nc.sync.dma_start(cls_sb[:], cls)
         nc.sync.dma_start(offs_sb[:], offs)
         for raw, c in zip(row2_raw, spans(ROW2_WIDTHS)):
             nc.sync.dma_start(raw[:], x_rows[:, 2, c])
-        for raw, c in zip(pair_raw, spans(PAIR_WIDTHS)):
-            nc.sync.dma_start(raw[:], x_rows[:, 0:2, c])
-        for raw, c in zip(row3_raw, spans(ROW3_WIDTHS)):
-            nc.sync.dma_start(raw[:], x_rows[:, 3, c])
         nc.sync.dma_start(beta_sb[:], beta)
-
-        w_codes = keep.tile([P, 2 * N], U8, name="w_codes", align_bytes=64)
-        w_scales = keep.tile([P, N], U8, name="w_scales", align_bytes=64)
-        nc.gpsimd.memset(w_scales[:], 0)
-        nc.gpsimd.dma_start(w_codes[:].bitcast(I32), w1_words[0].bitcast(I32))
+        nc.sync.dma_start(pair_raw[0][:], x_rows[:, 0:2, spans(PAIR_WIDTHS)[0]])
+        nc.sync.dma_start(w_codes[:].bitcast(I32), w1_words[0].bitcast(I32))
         for quad in range(4):
-            nc.gpsimd.dma_start(
+            nc.sync.dma_start(
                 w_scales[32 * quad : 32 * quad + 4, :].bitcast(I32),
                 w1_scales[0, 4 * quad : 4 * quad + 4, :].bitcast(I32),
             )
+        for raw, c in zip(pair_raw[1:], spans(PAIR_WIDTHS)[1:]):
+            nc.sync.dma_start(raw[:], x_rows[:, 0:2, c])
+        for raw, c in zip(row3_raw, spans(ROW3_WIDTHS)):
+            nc.sync.dma_start(raw[:], x_rows[:, 3, c])
 
         def entries(lst, first, count):
             return lst[:, first // STRIPE : (first + count) // STRIPE]
@@ -79,6 +79,10 @@ def tile_picked_cbn_none_e_kernel(tc, xT, w1_words, w1_scales, gamma, beta, offs
         gamma_picked = keep.tile([P, S], F32, name="gamma_picked")
         for first in range(0, S, 512):
             nc.vector.tensor_copy(gamma_picked[:, first : first + 512], gamma_sb[:].indirect(entries(cls_sb, first, 512)))
+
+        beta_picked = keep.tile([P, S], F32, name="beta_picked")
+        for first in range(0, S, 512):
+            nc.vector.tensor_copy(beta_picked[:, first : first + 512], beta_sb[:].indirect(entries(cls_sb, first, 512)))
 
         row2 = keep.tile([P, T], BF16, name="row2")
         row3 = keep.tile([P, T], BF16, name="row3")
@@ -103,7 +107,7 @@ def tile_picked_cbn_none_e_kernel(tc, xT, w1_words, w1_scales, gamma, beta, offs
             nc.scalar.activation(picked[i][:, :, 3], row3[:].indirect(entries(offs_sb, i * CHUNK, CHUNK)), COPY)
 
         def quantise_and_multiply(i):
-            codes = keep.tile([P, CHUNK], U32, name=f"codes{i}", tag=f"slot{i}", align_bytes=64)
+            codes = keep.tile([P, CHUNK], U32, name=f"codes{i}", tag=f"codes_slot{i % 2}", align_bytes=64)
             scales = keep.tile([P, CHUNK], U8, name=f"scales{i}", align_bytes=64)
             nc.vector.quantize_mx(out=codes[:].bitcast(FP8X4), scales=scales[:], in_=picked[i][:].rearrange("p s j -> p (s j)"))
             acc = psum.tile([P, CHUNK], F32, name=f"acc{i}")
@@ -119,14 +123,24 @@ def tile_picked_cbn_none_e_kernel(tc, xT, w1_words, w1_scales, gamma, beta, offs
             return acc
 
         def scale(i, acc):
-            scaled = keep.tile([P, CHUNK], F32, name=f"scaled{i}", tag=f"slot{i + 2}", align_bytes=64)
+            scaled = keep.tile([P, CHUNK], F32, name=f"scaled{i}")
             nc.vector.tensor_tensor(scaled[:], acc[:], gamma_picked[:, i * CHUNK : (i + 1) * CHUNK], MULT)
             return scaled
 
         def shift_and_store(i, scaled):
             result = keep.tile([P, CHUNK], F32, name=f"result{i}")
-            nc.vector.tensor_tensor(result[:], beta_sb[:].indirect(entries(cls_sb, i * CHUNK, CHUNK)), scaled[:], ADD)
+            nc.vector.tensor_tensor(result[:], scaled[:], beta_picked[:, i * CHUNK : (i + 1) * CHUNK], ADD)
             nc.sync.dma_start(out[:, i * CHUNK : (i + 1) * CHUNK], result[:])
 
-        for i in range(chunks):
-            shift_and_store(i, scale(i, quantise_and_multiply(i)))
+        acc0 = quantise_and_multiply(0)
+        acc1 = quantise_and_multiply(1)
+        scaled0 = scale(0, acc0)
+        acc2 = quantise_and_multiply(2)
+        shift_and_store(0, scaled0)
+        acc3 = quantise_and_multiply(3)
+        scaled1 = scale(1, acc1)
+        scaled2 = scale(2, acc2)
+        shift_and_store(1, scaled1)
+        scaled3 = scale(3, acc3)
+        shift_and_store(2, scaled2)
+        shift_and_store(3, scaled3)

@@ -21,7 +21,6 @@ P = 128
 PACK = 4
 STRIPE = 16
 CHUNK = 256
-ROW2_WIDTHS = (2048,)
 PAIR_WIDTHS = (1024, 640, 384)
 ROW3_WIDTHS = (512, 512, 512, 512)
 
@@ -48,9 +47,9 @@ def tile_picked_cbn_none_e_kernel(tc, xT, w1_words, w1_scales, gamma, beta, offs
         cls_sb = keep.tile([P, S // STRIPE], U16, name="cls_sb")
         gamma_sb = keep.tile([P, U], F32, name="gamma_sb")
         beta_sb = keep.tile([P, U], F32, name="beta_sb")
-        row2_raw = [keep.tile([P, c.stop - c.start], F32, name=f"row2_raw{i}") for i, c in enumerate(spans(ROW2_WIDTHS))]
+        row2_raw = keep.tile([P, T], F32, name="row2_raw")
         pair_raw = [keep.tile([P, 2, c.stop - c.start], F32, name=f"pair_raw{i}") for i, c in enumerate(spans(PAIR_WIDTHS))]
-        row3_raw = [keep.tile([P, c.stop - c.start], F32, name=f"row3_raw{i}") for i, c in enumerate(spans(ROW3_WIDTHS))]
+        row3_raw = keep.tile([P, T], F32, name="row3_raw")
 
         w_codes = keep.tile([P, 2 * N], U8, name="w_codes", align_bytes=64)
         w_scales = keep.tile([P, N], U8, name="w_scales", align_bytes=64)
@@ -58,20 +57,18 @@ def tile_picked_cbn_none_e_kernel(tc, xT, w1_words, w1_scales, gamma, beta, offs
         nc.sync.dma_start(gamma_sb[:], gamma)
         nc.sync.dma_start(cls_sb[:], cls)
         nc.sync.dma_start(offs_sb[:], offs)
-        for raw, c in zip(row2_raw, spans(ROW2_WIDTHS)):
-            nc.sync.dma_start(raw[:], x_rows[:, 2, c])
+        nc.sync.dma_start(row2_raw[:], x_rows[:, 2, :])
         nc.sync.dma_start(beta_sb[:], beta)
-        nc.sync.dma_start(pair_raw[0][:], x_rows[:, 0:2, spans(PAIR_WIDTHS)[0]])
         nc.sync.dma_start(w_codes[:].bitcast(I32), w1_words[0].bitcast(I32))
         for quad in range(4):
             nc.sync.dma_start(
                 w_scales[32 * quad : 32 * quad + 4, :].bitcast(I32),
                 w1_scales[0, 4 * quad : 4 * quad + 4, :].bitcast(I32),
             )
-        for raw, c in zip(pair_raw[1:], spans(PAIR_WIDTHS)[1:]):
+        for raw, c in zip(pair_raw, spans(PAIR_WIDTHS)):
             nc.sync.dma_start(raw[:], x_rows[:, 0:2, c])
-        for raw, c in zip(row3_raw, spans(ROW3_WIDTHS)):
-            nc.sync.dma_start(raw[:], x_rows[:, 3, c])
+        for c in spans(ROW3_WIDTHS):
+            nc.sync.dma_start(row3_raw[:, c], x_rows[:, 3, c])
 
         def entries(lst, first, count):
             return lst[:, first // STRIPE : (first + count) // STRIPE]
@@ -89,10 +86,12 @@ def tile_picked_cbn_none_e_kernel(tc, xT, w1_words, w1_scales, gamma, beta, offs
         pair = keep.tile([P, T, 2], BF16, name="pair")
         picked = [keep.tile([P, CHUNK, PACK], BF16, name=f"picked{i}", align_bytes=64) for i in range(chunks)]
 
-        for raw, c in zip(row2_raw, spans(ROW2_WIDTHS)):
-            nc.scalar.activation(row2[:, c], raw[:], COPY)
-        for i in range(chunks):
-            nc.scalar.activation(picked[i][:, :, 2], row2[:].indirect(entries(offs_sb, i * CHUNK, CHUNK)), COPY)
+        def gather_row(j, rounded):
+            for i in range(chunks):
+                nc.scalar.activation(picked[i][:, :, j], rounded[:].indirect(entries(offs_sb, i * CHUNK, CHUNK)), COPY)
+
+        nc.scalar.activation(row2[:], row2_raw[:], COPY)
+        gather_row(2, row2)
 
         for raw, c in zip(pair_raw, spans(PAIR_WIDTHS)):
             nc.vector.tensor_copy(pair[:, c, :], raw[:].rearrange("p j t -> p t j"))
@@ -101,46 +100,55 @@ def tile_picked_cbn_none_e_kernel(tc, xT, w1_words, w1_scales, gamma, beta, offs
             words = picked[i][:].rearrange("p s j -> p (s j)").bitcast(U32)
             nc.vector.tensor_copy(words[:, 0 : 2 * CHUNK : 2], pair_words.indirect(entries(offs_sb, i * CHUNK, CHUNK)))
 
-        for raw, c in zip(row3_raw, spans(ROW3_WIDTHS)):
-            nc.scalar.activation(row3[:, c], raw[:], COPY)
-        for i in range(chunks):
-            nc.scalar.activation(picked[i][:, :, 3], row3[:].indirect(entries(offs_sb, i * CHUNK, CHUNK)), COPY)
+        for c in spans(ROW3_WIDTHS):
+            nc.scalar.activation(row3[:, c], row3_raw[:, c], COPY)
+        gather_row(3, row3)
 
-        def quantise_and_multiply(i):
+        def quantise_and_multiply(i, parts):
             codes = keep.tile([P, CHUNK], U32, name=f"codes{i}", tag=f"codes_slot{i % 2}", align_bytes=64)
             scales = keep.tile([P, CHUNK], U8, name=f"scales{i}", align_bytes=64)
-            nc.vector.quantize_mx(out=codes[:].bitcast(FP8X4), scales=scales[:], in_=picked[i][:].rearrange("p s j -> p (s j)"))
-            acc = psum.tile([P, CHUNK], F32, name=f"acc{i}")
-            nc.tensor.matmul_mx(
-                out=acc[:],
-                lhsT=w_codes[:].bitcast(FP4X4),
-                lhsT_scale=w_scales[:],
-                rhs=codes[:].bitcast(FP8X4),
-                rhs_scale=scales[:],
-                start=True,
-                stop=True,
-            )
-            return acc
+            pieces = []
+            for part in spans([CHUNK // parts] * parts):
+                nc.vector.quantize_mx(
+                    out=codes[:, part].bitcast(FP8X4),
+                    scales=scales[:, part],
+                    in_=picked[i][:, part, :].rearrange("p s j -> p (s j)"),
+                )
+                columns = slice(i * CHUNK + part.start, i * CHUNK + part.stop)
+                acc = psum.tile([P, CHUNK // parts], F32, name=f"acc{columns.start}")
+                nc.tensor.matmul_mx(
+                    out=acc[:],
+                    lhsT=w_codes[:].bitcast(FP4X4),
+                    lhsT_scale=w_scales[:],
+                    rhs=codes[:, part].bitcast(FP8X4),
+                    rhs_scale=scales[:, part],
+                    start=True,
+                    stop=True,
+                )
+                pieces.append((columns, acc))
+            return pieces
 
-        def scale(i, acc):
-            scaled = keep.tile([P, CHUNK], F32, name=f"scaled{i}")
-            nc.vector.tensor_tensor(scaled[:], acc[:], gamma_picked[:, i * CHUNK : (i + 1) * CHUNK], MULT)
-            return scaled
+        def scale(columns, acc):
+            scaled = keep.tile([P, columns.stop - columns.start], F32, name=f"scaled{columns.start}")
+            nc.vector.tensor_tensor(scaled[:], acc[:], gamma_picked[:, columns], MULT)
+            return columns, scaled
 
-        def shift_and_store(i, scaled):
-            result = keep.tile([P, CHUNK], F32, name=f"result{i}")
-            nc.vector.tensor_tensor(result[:], scaled[:], beta_picked[:, i * CHUNK : (i + 1) * CHUNK], ADD)
-            nc.sync.dma_start(out[:, i * CHUNK : (i + 1) * CHUNK], result[:])
+        def shift_and_store(columns, scaled):
+            result = keep.tile([P, columns.stop - columns.start], F32, name=f"result{columns.start}")
+            nc.vector.tensor_tensor(result[:], scaled[:], beta_picked[:, columns], ADD)
+            nc.sync.dma_start(out[:, columns], result[:])
 
-        acc0 = quantise_and_multiply(0)
-        acc1 = quantise_and_multiply(1)
-        scaled0 = scale(0, acc0)
-        acc2 = quantise_and_multiply(2)
-        shift_and_store(0, scaled0)
-        acc3 = quantise_and_multiply(3)
-        scaled1 = scale(1, acc1)
-        scaled2 = scale(2, acc2)
-        shift_and_store(1, scaled1)
-        scaled3 = scale(3, acc3)
-        shift_and_store(2, scaled2)
-        shift_and_store(3, scaled3)
+        (acc0,) = quantise_and_multiply(0, 1)
+        (acc1,) = quantise_and_multiply(1, 1)
+        scaled0 = scale(*acc0)
+        (acc2,) = quantise_and_multiply(2, 1)
+        shift_and_store(*scaled0)
+        scaled1 = scale(*acc1)
+        acc3, acc4 = quantise_and_multiply(3, 2)
+        shift_and_store(*scaled1)
+        scaled2 = scale(*acc2)
+        scaled3 = scale(*acc3)
+        shift_and_store(*scaled2)
+        scaled4 = scale(*acc4)
+        shift_and_store(*scaled3)
+        shift_and_store(*scaled4)

@@ -21,6 +21,9 @@ P = 128
 PACK = 4
 STRIPE = 16
 CHUNK = 256
+ROW2_WIDTHS = (1024, 1024)
+SCALAR_SHARE = 128
+RUN = 4
 PAIR_WIDTHS = (1024, 640, 384)
 ROW3_WIDTHS = (512, 512, 512, 512)
 
@@ -57,8 +60,9 @@ def tile_picked_cbn_none_e_kernel(tc, xT, w1_words, w1_scales, gamma, beta, offs
         nc.sync.dma_start(gamma_sb[:], gamma)
         nc.sync.dma_start(cls_sb[:], cls)
         nc.sync.dma_start(offs_sb[:], offs)
-        nc.sync.dma_start(row2_raw[:], x_rows[:, 2, :])
         nc.sync.dma_start(beta_sb[:], beta)
+        for c in spans(ROW2_WIDTHS):
+            nc.sync.dma_start(row2_raw[:, c], x_rows[:, 2, c])
         nc.sync.dma_start(w_codes[:].bitcast(I32), w1_words[0].bitcast(I32))
         for quad in range(4):
             nc.sync.dma_start(
@@ -90,11 +94,21 @@ def tile_picked_cbn_none_e_kernel(tc, xT, w1_words, w1_scales, gamma, beta, offs
             for i in range(chunks):
                 nc.scalar.activation(picked[i][:, :, j], rounded[:].indirect(entries(offs_sb, i * CHUNK, CHUNK)), COPY)
 
-        nc.scalar.activation(row2[:], row2_raw[:], COPY)
+        for c in spans(ROW2_WIDTHS):
+            nc.scalar.activation(row2[:, c], row2_raw[:, c], COPY)
         gather_row(2, row2)
 
+        def pair_views(raw, first, count, place):
+            target = pair[:, place + first : place + first + count, :].rearrange("p (c i) j -> p c j i", i=RUN)
+            source = raw[:, :, first : first + count].rearrange("p j (c i) -> p c j i", i=RUN)
+            return target, source
+
         for raw, c in zip(pair_raw, spans(PAIR_WIDTHS)):
-            nc.vector.tensor_copy(pair[:, c, :], raw[:].rearrange("p j t -> p t j"))
+            width = c.stop - c.start
+            share = SCALAR_SHARE if c.stop == T else 0
+            nc.vector.tensor_copy(*pair_views(raw, 0, width - share, c.start))
+            if share:
+                nc.scalar.activation(*pair_views(raw, width - share, share, c.start), COPY)
         pair_words = pair[:].rearrange("p t j -> p (t j)").bitcast(U32)
         for i in range(chunks):
             words = picked[i][:].rearrange("p s j -> p (s j)").bitcast(U32)

@@ -19,12 +19,16 @@ ADD = mybir.AluOpType.add
 
 P = 128
 PACK = 4
+QUADRANT = 32
+SCALE_ROWS = 4
 STRIPE = 16
+CLASS_STEP = 512
 CHUNK = 256
-ROW2_WIDTHS = (1024, 1024)
-SCALAR_SHARE = 128
+LAST_PARTS = 2
+CODE_SLOTS = 2
 RUN = 4
-PAIR_WIDTHS = (1024, 640, 384)
+PAIR_WIDTHS = (1280, 768)
+SCALAR_SHARE = 192
 ROW3_WIDTHS = (512, 512, 512, 512)
 
 
@@ -35,6 +39,10 @@ def spans(widths):
         result.append(slice(start, start + width))
         start = start + width
     return result
+
+
+def entries(list_tile, first, count):
+    return list_tile[:, first // STRIPE : (first + count) // STRIPE]
 
 
 def tile_picked_cbn_none_e_kernel(tc, xT, w1_words, w1_scales, gamma, beta, offs, cls, out):
@@ -53,37 +61,37 @@ def tile_picked_cbn_none_e_kernel(tc, xT, w1_words, w1_scales, gamma, beta, offs
         row2_raw = keep.tile([P, T], F32, name="row2_raw")
         pair_raw = [keep.tile([P, 2, c.stop - c.start], F32, name=f"pair_raw{i}") for i, c in enumerate(spans(PAIR_WIDTHS))]
         row3_raw = keep.tile([P, T], F32, name="row3_raw")
-
         w_codes = keep.tile([P, 2 * N], U8, name="w_codes", align_bytes=64)
         w_scales = keep.tile([P, N], U8, name="w_scales", align_bytes=64)
+
         nc.gpsimd.memset(w_scales[:], 0)
+
         nc.sync.dma_start(gamma_sb[:], gamma)
         nc.sync.dma_start(cls_sb[:], cls)
         nc.sync.dma_start(offs_sb[:], offs)
+        nc.sync.dma_start(row2_raw[:], x_rows[:, 2, :])
         nc.sync.dma_start(beta_sb[:], beta)
-        for c in spans(ROW2_WIDTHS):
-            nc.sync.dma_start(row2_raw[:, c], x_rows[:, 2, c])
         nc.sync.dma_start(w_codes[:].bitcast(I32), w1_words[0].bitcast(I32))
-        for quad in range(4):
+        for quad in range(P // QUADRANT):
             nc.sync.dma_start(
-                w_scales[32 * quad : 32 * quad + 4, :].bitcast(I32),
-                w1_scales[0, 4 * quad : 4 * quad + 4, :].bitcast(I32),
+                w_scales[QUADRANT * quad : QUADRANT * quad + SCALE_ROWS, :].bitcast(I32),
+                w1_scales[0, SCALE_ROWS * quad : SCALE_ROWS * (quad + 1), :].bitcast(I32),
             )
         for raw, c in zip(pair_raw, spans(PAIR_WIDTHS)):
             nc.sync.dma_start(raw[:], x_rows[:, 0:2, c])
         for c in spans(ROW3_WIDTHS):
             nc.sync.dma_start(row3_raw[:, c], x_rows[:, 3, c])
 
-        def entries(lst, first, count):
-            return lst[:, first // STRIPE : (first + count) // STRIPE]
+        def gather_by_class(table, name):
+            looked_up = keep.tile([P, S], F32, name=name)
+            for first in range(0, S, CLASS_STEP):
+                nc.vector.tensor_copy(
+                    looked_up[:, first : first + CLASS_STEP], table[:].indirect(entries(cls_sb, first, CLASS_STEP))
+                )
+            return looked_up
 
-        gamma_picked = keep.tile([P, S], F32, name="gamma_picked")
-        for first in range(0, S, 512):
-            nc.vector.tensor_copy(gamma_picked[:, first : first + 512], gamma_sb[:].indirect(entries(cls_sb, first, 512)))
-
-        beta_picked = keep.tile([P, S], F32, name="beta_picked")
-        for first in range(0, S, 512):
-            nc.vector.tensor_copy(beta_picked[:, first : first + 512], beta_sb[:].indirect(entries(cls_sb, first, 512)))
+        gamma_picked = gather_by_class(gamma_sb, "gamma_picked")
+        beta_picked = gather_by_class(beta_sb, "beta_picked")
 
         row2 = keep.tile([P, T], BF16, name="row2")
         row3 = keep.tile([P, T], BF16, name="row3")
@@ -94,11 +102,10 @@ def tile_picked_cbn_none_e_kernel(tc, xT, w1_words, w1_scales, gamma, beta, offs
             for i in range(chunks):
                 nc.scalar.activation(picked[i][:, :, j], rounded[:].indirect(entries(offs_sb, i * CHUNK, CHUNK)), COPY)
 
-        for c in spans(ROW2_WIDTHS):
-            nc.scalar.activation(row2[:, c], row2_raw[:, c], COPY)
+        nc.scalar.activation(row2[:], row2_raw[:], COPY)
         gather_row(2, row2)
 
-        def pair_views(raw, first, count, place):
+        def pair_views(raw, place, first, count):
             target = pair[:, place + first : place + first + count, :].rearrange("p (c i) j -> p c j i", i=RUN)
             source = raw[:, :, first : first + count].rearrange("p j (c i) -> p c j i", i=RUN)
             return target, source
@@ -106,22 +113,26 @@ def tile_picked_cbn_none_e_kernel(tc, xT, w1_words, w1_scales, gamma, beta, offs
         for raw, c in zip(pair_raw, spans(PAIR_WIDTHS)):
             width = c.stop - c.start
             share = SCALAR_SHARE if c.stop == T else 0
-            nc.vector.tensor_copy(*pair_views(raw, 0, width - share, c.start))
+            nc.vector.tensor_copy(*pair_views(raw, c.start, 0, width - share))
             if share:
-                nc.scalar.activation(*pair_views(raw, width - share, share, c.start), COPY)
+                nc.scalar.activation(*pair_views(raw, c.start, width - share, share), COPY)
+
         pair_words = pair[:].rearrange("p t j -> p (t j)").bitcast(U32)
         for i in range(chunks):
-            words = picked[i][:].rearrange("p s j -> p (s j)").bitcast(U32)
-            nc.vector.tensor_copy(words[:, 0 : 2 * CHUNK : 2], pair_words.indirect(entries(offs_sb, i * CHUNK, CHUNK)))
+            picked_words = picked[i][:].rearrange("p s j -> p (s j)").bitcast(U32)
+            nc.vector.tensor_copy(
+                picked_words[:, 0 : 2 * CHUNK : 2], pair_words.indirect(entries(offs_sb, i * CHUNK, CHUNK))
+            )
 
         for c in spans(ROW3_WIDTHS):
             nc.scalar.activation(row3[:, c], row3_raw[:, c], COPY)
         gather_row(3, row3)
 
-        def quantise_and_multiply(i, parts):
-            codes = keep.tile([P, CHUNK], U32, name=f"codes{i}", tag=f"codes_slot{i % 2}", align_bytes=64)
+        def quantise_and_multiply(i):
+            parts = LAST_PARTS if i == chunks - 1 else 1
+            codes = keep.tile([P, CHUNK], U32, name=f"codes{i}", tag=f"codes_slot{i % CODE_SLOTS}", align_bytes=64)
             scales = keep.tile([P, CHUNK], U8, name=f"scales{i}", align_bytes=64)
-            pieces = []
+            products = []
             for part in spans([CHUNK // parts] * parts):
                 nc.vector.quantize_mx(
                     out=codes[:, part].bitcast(FP8X4),
@@ -139,8 +150,8 @@ def tile_picked_cbn_none_e_kernel(tc, xT, w1_words, w1_scales, gamma, beta, offs
                     start=True,
                     stop=True,
                 )
-                pieces.append((columns, acc))
-            return pieces
+                products.append((columns, acc))
+            return products
 
         def scale(columns, acc):
             scaled = keep.tile([P, columns.stop - columns.start], F32, name=f"scaled{columns.start}")
@@ -152,17 +163,16 @@ def tile_picked_cbn_none_e_kernel(tc, xT, w1_words, w1_scales, gamma, beta, offs
             nc.vector.tensor_tensor(result[:], scaled[:], beta_picked[:, columns], ADD)
             nc.sync.dma_start(out[:, columns], result[:])
 
-        (acc0,) = quantise_and_multiply(0, 1)
-        (acc1,) = quantise_and_multiply(1, 1)
-        scaled0 = scale(*acc0)
-        (acc2,) = quantise_and_multiply(2, 1)
-        shift_and_store(*scaled0)
-        scaled1 = scale(*acc1)
-        acc3, acc4 = quantise_and_multiply(3, 2)
-        shift_and_store(*scaled1)
-        scaled2 = scale(*acc2)
-        scaled3 = scale(*acc3)
-        shift_and_store(*scaled2)
-        scaled4 = scale(*acc4)
-        shift_and_store(*scaled3)
-        shift_and_store(*scaled4)
+        products = []
+        for i in range(CODE_SLOTS):
+            products.extend(quantise_and_multiply(i))
+        for i in range(chunks - CODE_SLOTS):
+            scaled = scale(*products[i])
+            products.extend(quantise_and_multiply(i + CODE_SLOTS))
+            shift_and_store(*scaled)
+        waiting = scale(*products[chunks - CODE_SLOTS])
+        for product in products[chunks - CODE_SLOTS + 1 :]:
+            scaled = scale(*product)
+            shift_and_store(*waiting)
+            waiting = scaled
+        shift_and_store(*waiting)

@@ -29,6 +29,7 @@ CODE_SLOTS = 2
 RUN = 4
 PAIR_WIDTHS = (1280, 768)
 SCALAR_SHARE = 192
+ROW2_WIDTHS = (1024, 1024)
 ROW3_WIDTHS = (512, 512, 512, 512)
 
 
@@ -69,18 +70,19 @@ def tile_picked_cbn_none_e_kernel(tc, xT, w1_words, w1_scales, gamma, beta, offs
         nc.sync.dma_start(gamma_sb[:], gamma)
         nc.sync.dma_start(cls_sb[:], cls)
         nc.sync.dma_start(offs_sb[:], offs)
-        nc.sync.dma_start(row2_raw[:], x_rows[:, 2, :])
+        for c in spans(ROW2_WIDTHS):
+            nc.sync.dma_start(row2_raw[:, c], x_rows[:, 2, c])
         nc.sync.dma_start(beta_sb[:], beta)
+        for raw, c in zip(pair_raw, spans(PAIR_WIDTHS)):
+            nc.sync.dma_start(raw[:], x_rows[:, 0:2, c])
+        for c in spans(ROW3_WIDTHS):
+            nc.sync.dma_start(row3_raw[:, c], x_rows[:, 3, c])
         nc.sync.dma_start(w_codes[:].bitcast(I32), w1_words[0].bitcast(I32))
         for quad in range(P // QUADRANT):
             nc.sync.dma_start(
                 w_scales[QUADRANT * quad : QUADRANT * quad + SCALE_ROWS, :].bitcast(I32),
                 w1_scales[0, SCALE_ROWS * quad : SCALE_ROWS * (quad + 1), :].bitcast(I32),
             )
-        for raw, c in zip(pair_raw, spans(PAIR_WIDTHS)):
-            nc.sync.dma_start(raw[:], x_rows[:, 0:2, c])
-        for c in spans(ROW3_WIDTHS):
-            nc.sync.dma_start(row3_raw[:, c], x_rows[:, 3, c])
 
         def gather_by_class(table, name):
             looked_up = keep.tile([P, S], F32, name=name)
@@ -91,9 +93,12 @@ def tile_picked_cbn_none_e_kernel(tc, xT, w1_words, w1_scales, gamma, beta, offs
             return looked_up
 
         gamma_picked = gather_by_class(gamma_sb, "gamma_picked")
+        row2 = keep.tile([P, T], BF16, name="row2")
+        early, late = spans(ROW2_WIDTHS)
+        nc.scalar.activation(row2[:, early], row2_raw[:, early], COPY)
+        nc.vector.tensor_copy(row2[:, late], row2_raw[:, late])
         beta_picked = gather_by_class(beta_sb, "beta_picked")
 
-        row2 = keep.tile([P, T], BF16, name="row2")
         row3 = keep.tile([P, T], BF16, name="row3")
         pair = keep.tile([P, T, 2], BF16, name="pair")
         picked = [keep.tile([P, CHUNK, PACK], BF16, name=f"picked{i}", align_bytes=64) for i in range(chunks)]
@@ -102,7 +107,6 @@ def tile_picked_cbn_none_e_kernel(tc, xT, w1_words, w1_scales, gamma, beta, offs
             for i in range(chunks):
                 nc.scalar.activation(picked[i][:, :, j], rounded[:].indirect(entries(offs_sb, i * CHUNK, CHUNK)), COPY)
 
-        nc.scalar.activation(row2[:], row2_raw[:], COPY)
         gather_row(2, row2)
 
         def pair_views(raw, place, first, count):

@@ -27,10 +27,11 @@ CHUNK = 256
 LAST_PARTS = 2
 CODE_SLOTS = 2
 RUN = 4
-PAIR_WIDTHS = (1280, 768)
-SCALAR_SHARE = 192
-ROW2_WIDTHS = (1024, 1024)
-ROW3_WIDTHS = (512, 512, 512, 512)
+PAIR_WIDTHS = (768, 768, 512)
+SCALAR_SHARES = (768, 320, 160)
+VECTOR_CHUNK = 0
+ROW2_WIDTHS = (512, 512, 512, 512)
+ROW3_WIDTHS = (640, 640, 768)
 
 
 def spans(widths):
@@ -70,11 +71,11 @@ def tile_picked_cbn_none_e_kernel(tc, xT, w1_words, w1_scales, gamma, beta, offs
         nc.sync.dma_start(gamma_sb[:], gamma)
         nc.sync.dma_start(cls_sb[:], cls)
         nc.sync.dma_start(offs_sb[:], offs)
-        for c in spans(ROW2_WIDTHS):
-            nc.sync.dma_start(row2_raw[:, c], x_rows[:, 2, c])
         nc.sync.dma_start(beta_sb[:], beta)
         for raw, c in zip(pair_raw, spans(PAIR_WIDTHS)):
             nc.sync.dma_start(raw[:], x_rows[:, 0:2, c])
+        for c in spans(ROW2_WIDTHS):
+            nc.sync.dma_start(row2_raw[:, c], x_rows[:, 2, c])
         for c in spans(ROW3_WIDTHS):
             nc.sync.dma_start(row3_raw[:, c], x_rows[:, 3, c])
         nc.sync.dma_start(w_codes[:].bitcast(I32), w1_words[0].bitcast(I32))
@@ -94,32 +95,30 @@ def tile_picked_cbn_none_e_kernel(tc, xT, w1_words, w1_scales, gamma, beta, offs
 
         gamma_picked = gather_by_class(gamma_sb, "gamma_picked")
         row2 = keep.tile([P, T], BF16, name="row2")
-        early, late = spans(ROW2_WIDTHS)
-        nc.scalar.activation(row2[:, early], row2_raw[:, early], COPY)
-        nc.vector.tensor_copy(row2[:, late], row2_raw[:, late])
         beta_picked = gather_by_class(beta_sb, "beta_picked")
 
         row3 = keep.tile([P, T], BF16, name="row3")
         pair = keep.tile([P, T, 2], BF16, name="pair")
         picked = [keep.tile([P, CHUNK, PACK], BF16, name=f"picked{i}", align_bytes=64) for i in range(chunks)]
 
-        def gather_row(j, rounded):
+        def gather_row(j, raw, rounded):
             for i in range(chunks):
-                nc.scalar.activation(picked[i][:, :, j], rounded[:].indirect(entries(offs_sb, i * CHUNK, CHUNK)), COPY)
-
-        gather_row(2, row2)
+                offsets = entries(offs_sb, i * CHUNK, CHUNK)
+                if i == VECTOR_CHUNK:
+                    nc.vector.tensor_copy(picked[i][:, :, j], raw[:].indirect(offsets))
+                else:
+                    nc.scalar.activation(picked[i][:, :, j], rounded[:].indirect(offsets), COPY)
 
         def pair_views(raw, place, first, count):
             target = pair[:, place + first : place + first + count, :].rearrange("p (c i) j -> p c j i", i=RUN)
             source = raw[:, :, first : first + count].rearrange("p j (c i) -> p c j i", i=RUN)
             return target, source
 
-        for raw, c in zip(pair_raw, spans(PAIR_WIDTHS)):
+        for raw, c, share in zip(pair_raw, spans(PAIR_WIDTHS), SCALAR_SHARES):
             width = c.stop - c.start
-            share = SCALAR_SHARE if c.stop == T else 0
-            nc.vector.tensor_copy(*pair_views(raw, c.start, 0, width - share))
-            if share:
-                nc.scalar.activation(*pair_views(raw, c.start, width - share, share), COPY)
+            if share < width:
+                nc.vector.tensor_copy(*pair_views(raw, c.start, 0, width - share))
+            nc.scalar.activation(*pair_views(raw, c.start, width - share, share), COPY)
 
         pair_words = pair[:].rearrange("p t j -> p (t j)").bitcast(U32)
         for i in range(chunks):
@@ -128,9 +127,14 @@ def tile_picked_cbn_none_e_kernel(tc, xT, w1_words, w1_scales, gamma, beta, offs
                 picked_words[:, 0 : 2 * CHUNK : 2], pair_words.indirect(entries(offs_sb, i * CHUNK, CHUNK))
             )
 
-        for c in spans(ROW3_WIDTHS):
-            nc.scalar.activation(row3[:, c], row3_raw[:, c], COPY)
-        gather_row(3, row3)
+        for c in spans(ROW2_WIDTHS):
+            nc.scalar.activation(row2[:, c], row2_raw[:, c], COPY)
+        gather_row(2, row2_raw, row2)
+        *early, last = spans(ROW3_WIDTHS)
+        for c in early:
+            nc.gpsimd.tensor_scalar(row3[:, c], row3_raw[:, c], 1.0, 0.0, MULT, ADD)
+        nc.vector.tensor_copy(row3[:, last], row3_raw[:, last])
+        gather_row(3, row3_raw, row3)
 
         def quantise_and_multiply(i):
             parts = LAST_PARTS if i == chunks - 1 else 1

@@ -27,11 +27,11 @@ CHUNK = 256
 LAST_PARTS = 2
 CODE_SLOTS = 2
 RUN = 4
-PAIR_WIDTHS = (768, 768, 512)
-SCALAR_SHARES = (768, 320, 160)
+PAIR_WIDTHS = (1280, 768)
+SCALAR_SHARES = (736, 256)
 VECTOR_CHUNK = 0
-ROW2_WIDTHS = (512, 512, 512, 512)
-ROW3_WIDTHS = (640, 640, 768)
+ROW2_WIDTHS = (704, 672, 672)
+ROW3_WIDTHS = (512, 768, 768)
 
 
 def spans(widths):
@@ -130,10 +130,8 @@ def tile_picked_cbn_none_e_kernel(tc, xT, w1_words, w1_scales, gamma, beta, offs
         for c in spans(ROW2_WIDTHS):
             nc.scalar.activation(row2[:, c], row2_raw[:, c], COPY)
         gather_row(2, row2_raw, row2)
-        *early, last = spans(ROW3_WIDTHS)
-        for c in early:
+        for c in spans(ROW3_WIDTHS):
             nc.gpsimd.tensor_scalar(row3[:, c], row3_raw[:, c], 1.0, 0.0, MULT, ADD)
-        nc.vector.tensor_copy(row3[:, last], row3_raw[:, last])
         gather_row(3, row3_raw, row3)
 
         def quantise_and_multiply(i):

@@ -27,9 +27,11 @@ CHUNK = 256
 LAST_PARTS = 2
 CODE_SLOTS = 2
 RUN = 4
-PAIR_WIDTHS = (1280, 768)
-SCALAR_SHARES = (736, 256)
+PAIR_FIRST = slice(768, 1536)
+PAIR_PARTS = (PAIR_FIRST, slice(0, PAIR_FIRST.start), slice(PAIR_FIRST.stop, T))
+SCALAR_SHARES = (384, 256, 192)
 VECTOR_CHUNK = 0
+STAGED_CHUNK = 1
 ROW2_WIDTHS = (704, 672, 672)
 ROW3_WIDTHS = (512, 768, 768)
 
@@ -51,6 +53,7 @@ def tile_picked_cbn_none_e_kernel(tc, xT, w1_words, w1_scales, gamma, beta, offs
     nc = tc.nc
     chunks = S // CHUNK
     x_rows = xT.rearrange("(p j) t -> p j t", j=PACK)
+    x_flat = xT.rearrange("(p j) t -> p (j t)", j=PACK)
 
     with ExitStack() as ctx:
         keep = ctx.enter_context(tc.tile_pool(name="keep", bufs=1))
@@ -61,7 +64,7 @@ def tile_picked_cbn_none_e_kernel(tc, xT, w1_words, w1_scales, gamma, beta, offs
         gamma_sb = keep.tile([P, U], F32, name="gamma_sb")
         beta_sb = keep.tile([P, U], F32, name="beta_sb")
         row2_raw = keep.tile([P, T], F32, name="row2_raw")
-        pair_raw = [keep.tile([P, 2, c.stop - c.start], F32, name=f"pair_raw{i}") for i, c in enumerate(spans(PAIR_WIDTHS))]
+        pair_raw = keep.tile([P, 2 * T], F32, name="pair_raw")
         row3_raw = keep.tile([P, T], F32, name="row3_raw")
         w_codes = keep.tile([P, 2 * N], U8, name="w_codes", align_bytes=64)
         w_scales = keep.tile([P, N], U8, name="w_scales", align_bytes=64)
@@ -72,8 +75,8 @@ def tile_picked_cbn_none_e_kernel(tc, xT, w1_words, w1_scales, gamma, beta, offs
         nc.sync.dma_start(cls_sb[:], cls)
         nc.sync.dma_start(offs_sb[:], offs)
         nc.sync.dma_start(beta_sb[:], beta)
-        for raw, c in zip(pair_raw, spans(PAIR_WIDTHS)):
-            nc.sync.dma_start(raw[:], x_rows[:, 0:2, c])
+        for c in (slice(PAIR_FIRST.start, T + PAIR_FIRST.stop), slice(0, PAIR_FIRST.start), slice(T + PAIR_FIRST.stop, 2 * T)):
+            nc.sync.dma_start(pair_raw[:, c], x_flat[:, c])
         for c in spans(ROW2_WIDTHS):
             nc.sync.dma_start(row2_raw[:, c], x_rows[:, 2, c])
         for c in spans(ROW3_WIDTHS):
@@ -101,24 +104,25 @@ def tile_picked_cbn_none_e_kernel(tc, xT, w1_words, w1_scales, gamma, beta, offs
         pair = keep.tile([P, T, 2], BF16, name="pair")
         picked = [keep.tile([P, CHUNK, PACK], BF16, name=f"picked{i}", align_bytes=64) for i in range(chunks)]
 
+        staged = keep.tile([P, 2, CHUNK], BF16, name="staged")
+
         def gather_row(j, raw, rounded):
             for i in range(chunks):
                 offsets = entries(offs_sb, i * CHUNK, CHUNK)
-                if i == VECTOR_CHUNK:
-                    nc.vector.tensor_copy(picked[i][:, :, j], raw[:].indirect(offsets))
+                target = staged[:, j - 2, :] if i == STAGED_CHUNK else picked[i][:, :, j]
+                if i == VECTOR_CHUNK or (i == STAGED_CHUNK and j == 3):
+                    nc.vector.tensor_copy(target, raw[:].indirect(offsets))
                 else:
-                    nc.scalar.activation(picked[i][:, :, j], rounded[:].indirect(offsets), COPY)
+                    nc.scalar.activation(target, rounded[:].indirect(offsets), COPY)
 
-        def pair_views(raw, place, first, count):
-            target = pair[:, place + first : place + first + count, :].rearrange("p (c i) j -> p c j i", i=RUN)
-            source = raw[:, :, first : first + count].rearrange("p j (c i) -> p c j i", i=RUN)
-            return target, source
+        def pair_views(first, stop):
+            target = pair[:, first:stop, :].rearrange("p (c i) j -> p c j i", i=RUN)
+            rows = pair_raw[:].rearrange("p (j t) -> p j t", j=2)
+            return target, rows[:, :, first:stop].rearrange("p j (c i) -> p c j i", i=RUN)
 
-        for raw, c, share in zip(pair_raw, spans(PAIR_WIDTHS), SCALAR_SHARES):
-            width = c.stop - c.start
-            if share < width:
-                nc.vector.tensor_copy(*pair_views(raw, c.start, 0, width - share))
-            nc.scalar.activation(*pair_views(raw, c.start, width - share, share), COPY)
+        for c, share in zip(PAIR_PARTS, SCALAR_SHARES):
+            nc.vector.tensor_copy(*pair_views(c.start, c.stop - share))
+            nc.scalar.activation(*pair_views(c.stop - share, c.stop), COPY)
 
         pair_words = pair[:].rearrange("p t j -> p (t j)").bitcast(U32)
         for i in range(chunks):
@@ -133,6 +137,9 @@ def tile_picked_cbn_none_e_kernel(tc, xT, w1_words, w1_scales, gamma, beta, offs
         for c in spans(ROW3_WIDTHS):
             nc.gpsimd.tensor_scalar(row3[:, c], row3_raw[:, c], 1.0, 0.0, MULT, ADD)
         gather_row(3, row3_raw, row3)
+
+        def place_staged():
+            nc.vector.tensor_copy(picked[STAGED_CHUNK][:, :, 2:4], staged[:].rearrange("p j s -> p s j"))
 
         def quantise_and_multiply(i):
             parts = LAST_PARTS if i == chunks - 1 else 1
@@ -171,6 +178,8 @@ def tile_picked_cbn_none_e_kernel(tc, xT, w1_words, w1_scales, gamma, beta, offs
 
         products = []
         for i in range(CODE_SLOTS):
+            if i == STAGED_CHUNK:
+                place_staged()
             products.extend(quantise_and_multiply(i))
         for i in range(chunks - CODE_SLOTS):
             scaled = scale(*products[i])

@@ -25,20 +25,22 @@ STRIPE = 16
 CLASS_STEP = 512
 CHUNK = 256
 LAST_PARTS = 2
-CODE_SLOTS = 2
-RUN = 4
-PAIR_FIRST = slice(768, 1536)
-PAIR_PARTS = (PAIR_FIRST, slice(0, PAIR_FIRST.start), slice(PAIR_FIRST.stop, T))
-SCALAR_SHARES = (384, 256, 192)
-VECTOR_CHUNK = 0
-STAGED_CHUNK = 1
-ROW2_WIDTHS = (704, 672, 672)
-ROW3_WIDTHS = (512, 768, 768)
+GATHERS = {
+    2: (("vector", 512), ("scalar", 512)),
+    0: (("vector", 352), ("scalar", 672)),
+    1: (("vector", 352), ("scalar", 672)),
+    3: (("vector", 256), ("vector", 256), ("scalar", 256), ("scalar", 256)),
+}
+ROW_LOADS = {
+    2: ((("scalar", 1024),), (("gpsimd", 448), ("scalar", 576))),
+    0: ((("vector", 1408),), (("gpsimd", 640),)),
+    1: ((("vector", 1408),), (("gpsimd", 640),)),
+    3: ((("gpsimd", 640),), (("gpsimd", 384), ("scalar", 512)), (("gpsimd", 320), ("scalar", 192))),
+}
 
 
-def spans(widths):
+def spans(widths, start=0):
     result = []
-    start = 0
     for width in widths:
         result.append(slice(start, start + width))
         start = start + width
@@ -53,7 +55,6 @@ def tile_picked_cbn_none_e_kernel(tc, xT, w1_words, w1_scales, gamma, beta, offs
     nc = tc.nc
     chunks = S // CHUNK
     x_rows = xT.rearrange("(p j) t -> p j t", j=PACK)
-    x_flat = xT.rearrange("(p j) t -> p (j t)", j=PACK)
 
     with ExitStack() as ctx:
         keep = ctx.enter_context(tc.tile_pool(name="keep", bufs=1))
@@ -63,24 +64,29 @@ def tile_picked_cbn_none_e_kernel(tc, xT, w1_words, w1_scales, gamma, beta, offs
         cls_sb = keep.tile([P, S // STRIPE], U16, name="cls_sb")
         gamma_sb = keep.tile([P, U], F32, name="gamma_sb")
         beta_sb = keep.tile([P, U], F32, name="beta_sb")
-        row2_raw = keep.tile([P, T], F32, name="row2_raw")
-        pair_raw = keep.tile([P, 2 * T], F32, name="pair_raw")
-        row3_raw = keep.tile([P, T], F32, name="row3_raw")
+        raw = [keep.tile([P, T], F32, name=f"raw{j}") for j in range(PACK)]
+        rounded = [keep.tile([P, T], BF16, name=f"rounded{j}") for j in range(PACK)]
         w_codes = keep.tile([P, 2 * N], U8, name="w_codes", align_bytes=64)
         w_scales = keep.tile([P, N], U8, name="w_scales", align_bytes=64)
+        picked = keep.tile([P, S, PACK], BF16, name="picked", align_bytes=64)
 
         nc.gpsimd.memset(w_scales[:], 0)
+
+        def load_spans(j):
+            return spans([sum(width for engine, width in load) for load in ROW_LOADS[j]])
+
+        def load_row(j):
+            for c in load_spans(j):
+                nc.sync.dma_start(raw[j][:, c], x_rows[:, j, c])
 
         nc.sync.dma_start(gamma_sb[:], gamma)
         nc.sync.dma_start(cls_sb[:], cls)
         nc.sync.dma_start(offs_sb[:], offs)
+        load_row(2)
+        load_row(0)
+        load_row(1)
         nc.sync.dma_start(beta_sb[:], beta)
-        for c in (slice(PAIR_FIRST.start, T + PAIR_FIRST.stop), slice(0, PAIR_FIRST.start), slice(T + PAIR_FIRST.stop, 2 * T)):
-            nc.sync.dma_start(pair_raw[:, c], x_flat[:, c])
-        for c in spans(ROW2_WIDTHS):
-            nc.sync.dma_start(row2_raw[:, c], x_rows[:, 2, c])
-        for c in spans(ROW3_WIDTHS):
-            nc.sync.dma_start(row3_raw[:, c], x_rows[:, 3, c])
+        load_row(3)
         nc.sync.dma_start(w_codes[:].bitcast(I32), w1_words[0].bitcast(I32))
         for quad in range(P // QUADRANT):
             nc.sync.dma_start(
@@ -96,98 +102,70 @@ def tile_picked_cbn_none_e_kernel(tc, xT, w1_words, w1_scales, gamma, beta, offs
                 )
             return looked_up
 
-        gamma_picked = gather_by_class(gamma_sb, "gamma_picked")
-        row2 = keep.tile([P, T], BF16, name="row2")
-        beta_picked = gather_by_class(beta_sb, "beta_picked")
+        def round_row(j):
+            for load, load_span in zip(ROW_LOADS[j], load_spans(j)):
+                for (engine, width), c in zip(load, spans([width for engine, width in load], load_span.start)):
+                    if engine == "gpsimd":
+                        nc.gpsimd.tensor_scalar(rounded[j][:, c], raw[j][:, c], 1.0, 0.0, MULT, ADD)
+                    elif engine == "scalar":
+                        nc.scalar.activation(rounded[j][:, c], raw[j][:, c], COPY)
+                    else:
+                        nc.vector.tensor_copy(rounded[j][:, c], raw[j][:, c])
 
-        row3 = keep.tile([P, T], BF16, name="row3")
-        pair = keep.tile([P, T, 2], BF16, name="pair")
-        picked = [keep.tile([P, CHUNK, PACK], BF16, name=f"picked{i}", align_bytes=64) for i in range(chunks)]
-
-        staged = keep.tile([P, 2, CHUNK], BF16, name="staged")
-
-        def gather_row(j, raw, rounded):
-            for i in range(chunks):
-                offsets = entries(offs_sb, i * CHUNK, CHUNK)
-                target = staged[:, j - 2, :] if i == STAGED_CHUNK else picked[i][:, :, j]
-                if i == VECTOR_CHUNK or (i == STAGED_CHUNK and j == 3):
-                    nc.vector.tensor_copy(target, raw[:].indirect(offsets))
+        def gather_row(j):
+            for (engine, count), c in zip(GATHERS[j], spans([count for engine, count in GATHERS[j]])):
+                offsets = entries(offs_sb, c.start, count)
+                if engine == "vector":
+                    nc.vector.tensor_copy(picked[:, c, j], raw[j][:].indirect(offsets))
                 else:
-                    nc.scalar.activation(target, rounded[:].indirect(offsets), COPY)
+                    nc.scalar.activation(picked[:, c, j], rounded[j][:].indirect(offsets), COPY)
 
-        def pair_views(first, stop):
-            target = pair[:, first:stop, :].rearrange("p (c i) j -> p c j i", i=RUN)
-            rows = pair_raw[:].rearrange("p (j t) -> p j t", j=2)
-            return target, rows[:, :, first:stop].rearrange("p j (c i) -> p c j i", i=RUN)
-
-        for c, share in zip(PAIR_PARTS, SCALAR_SHARES):
-            nc.vector.tensor_copy(*pair_views(c.start, c.stop - share))
-            nc.scalar.activation(*pair_views(c.stop - share, c.stop), COPY)
-
-        pair_words = pair[:].rearrange("p t j -> p (t j)").bitcast(U32)
-        for i in range(chunks):
-            picked_words = picked[i][:].rearrange("p s j -> p (s j)").bitcast(U32)
-            nc.vector.tensor_copy(
-                picked_words[:, 0 : 2 * CHUNK : 2], pair_words.indirect(entries(offs_sb, i * CHUNK, CHUNK))
-            )
-
-        for c in spans(ROW2_WIDTHS):
-            nc.scalar.activation(row2[:, c], row2_raw[:, c], COPY)
-        gather_row(2, row2_raw, row2)
-        for c in spans(ROW3_WIDTHS):
-            nc.gpsimd.tensor_scalar(row3[:, c], row3_raw[:, c], 1.0, 0.0, MULT, ADD)
-        gather_row(3, row3_raw, row3)
-
-        def place_staged():
-            nc.vector.tensor_copy(picked[STAGED_CHUNK][:, :, 2:4], staged[:].rearrange("p j s -> p s j"))
+        gamma_picked = gather_by_class(gamma_sb, "gamma_picked")
+        for j in (2, 0, 1):
+            round_row(j)
+            gather_row(j)
+        beta_picked = gather_by_class(beta_sb, "beta_picked")
+        round_row(3)
+        gather_row(3)
 
         def quantise_and_multiply(i):
-            parts = LAST_PARTS if i == chunks - 1 else 1
-            codes = keep.tile([P, CHUNK], U32, name=f"codes{i}", tag=f"codes_slot{i % CODE_SLOTS}", align_bytes=64)
+            columns = slice(i * CHUNK, (i + 1) * CHUNK)
+            codes = keep.tile([P, CHUNK], U32, name=f"codes{i}", align_bytes=64)
             scales = keep.tile([P, CHUNK], U8, name=f"scales{i}", align_bytes=64)
-            products = []
+            nc.vector.quantize_mx(
+                out=codes[:].bitcast(FP8X4),
+                scales=scales[:],
+                in_=picked[:, columns, :].rearrange("p s j -> p (s j)"),
+            )
+            acc = psum.tile([P, CHUNK], F32, name=f"acc{i}")
+            nc.tensor.matmul_mx(
+                out=acc[:],
+                lhsT=w_codes[:].bitcast(FP4X4),
+                lhsT_scale=w_scales[:],
+                rhs=codes[:].bitcast(FP8X4),
+                rhs_scale=scales[:],
+                start=True,
+                stop=True,
+            )
+            return acc
+
+        def scale(i):
+            scaled = keep.tile([P, CHUNK], F32, name=f"scaled{i}")
+            nc.vector.tensor_tensor(scaled[:], products[i][:], gamma_picked[:, i * CHUNK : (i + 1) * CHUNK], MULT)
+            return scaled
+
+        def shift_and_store(i, scaled):
+            parts = LAST_PARTS if i == chunks - 1 else 1
+            result = keep.tile([P, CHUNK], F32, name=f"result{i}")
             for part in spans([CHUNK // parts] * parts):
-                nc.vector.quantize_mx(
-                    out=codes[:, part].bitcast(FP8X4),
-                    scales=scales[:, part],
-                    in_=picked[i][:, part, :].rearrange("p s j -> p (s j)"),
-                )
                 columns = slice(i * CHUNK + part.start, i * CHUNK + part.stop)
-                acc = psum.tile([P, CHUNK // parts], F32, name=f"acc{columns.start}")
-                nc.tensor.matmul_mx(
-                    out=acc[:],
-                    lhsT=w_codes[:].bitcast(FP4X4),
-                    lhsT_scale=w_scales[:],
-                    rhs=codes[:, part].bitcast(FP8X4),
-                    rhs_scale=scales[:, part],
-                    start=True,
-                    stop=True,
-                )
-                products.append((columns, acc))
-            return products
+                nc.vector.tensor_tensor(result[:, part], scaled[:, part], beta_picked[:, columns], ADD)
+                nc.sync.dma_start(out[:, columns], result[:, part])
 
-        def scale(columns, acc):
-            scaled = keep.tile([P, columns.stop - columns.start], F32, name=f"scaled{columns.start}")
-            nc.vector.tensor_tensor(scaled[:], acc[:], gamma_picked[:, columns], MULT)
-            return columns, scaled
-
-        def shift_and_store(columns, scaled):
-            result = keep.tile([P, columns.stop - columns.start], F32, name=f"result{columns.start}")
-            nc.vector.tensor_tensor(result[:], scaled[:], beta_picked[:, columns], ADD)
-            nc.sync.dma_start(out[:, columns], result[:])
-
-        products = []
-        for i in range(CODE_SLOTS):
-            if i == STAGED_CHUNK:
-                place_staged()
-            products.extend(quantise_and_multiply(i))
-        for i in range(chunks - CODE_SLOTS):
-            scaled = scale(*products[i])
-            products.extend(quantise_and_multiply(i + CODE_SLOTS))
-            shift_and_store(*scaled)
-        waiting = scale(*products[chunks - CODE_SLOTS])
-        for product in products[chunks - CODE_SLOTS + 1 :]:
-            scaled = scale(*product)
-            shift_and_store(*waiting)
+        products = [quantise_and_multiply(i) for i in range(chunks)]
+        waiting = scale(0)
+        for i in range(1, chunks):
+            scaled = scale(i)
+            shift_and_store(i - 1, waiting)
             waiting = scaled
-        shift_and_store(*waiting)
+        shift_and_store(chunks - 1, waiting)

@@ -32,7 +32,7 @@ GATHERS = {
     3: (("vector", 256), ("vector", 256), ("scalar", 256), ("scalar", 256)),
 }
 ROW_LOADS = {
-    2: ((("scalar", 1024),), (("gpsimd", 448), ("scalar", 576))),
+    2: ((("gpsimd", 960), ("scalar", 1088)),),
     0: ((("vector", 1408),), (("gpsimd", 640),)),
     1: ((("vector", 1408),), (("gpsimd", 640),)),
     3: ((("gpsimd", 640),), (("gpsimd", 384), ("scalar", 512)), (("gpsimd", 320), ("scalar", 192))),
@@ -149,23 +149,23 @@ def tile_picked_cbn_none_e_kernel(tc, xT, w1_words, w1_scales, gamma, beta, offs
             )
             return acc
 
-        def scale(i):
-            scaled = keep.tile([P, CHUNK], F32, name=f"scaled{i}")
-            nc.vector.tensor_tensor(scaled[:], products[i][:], gamma_picked[:, i * CHUNK : (i + 1) * CHUNK], MULT)
-            return scaled
+        def scale(i, part):
+            columns = slice(i * CHUNK + part.start, i * CHUNK + part.stop)
+            scaled = keep.tile([P, part.stop - part.start], F32, name=f"scaled{columns.start}")
+            nc.vector.tensor_tensor(scaled[:], products[i][:, part], gamma_picked[:, columns], MULT)
+            return columns, scaled
 
-        def shift_and_store(i, scaled):
-            parts = LAST_PARTS if i == chunks - 1 else 1
-            result = keep.tile([P, CHUNK], F32, name=f"result{i}")
-            for part in spans([CHUNK // parts] * parts):
-                columns = slice(i * CHUNK + part.start, i * CHUNK + part.stop)
-                nc.vector.tensor_tensor(result[:, part], scaled[:, part], beta_picked[:, columns], ADD)
-                nc.sync.dma_start(out[:, columns], result[:, part])
+        def shift_and_store(columns, scaled):
+            result = keep.tile([P, columns.stop - columns.start], F32, name=f"result{columns.start}")
+            nc.vector.tensor_tensor(result[:], scaled[:], beta_picked[:, columns], ADD)
+            nc.sync.dma_start(out[:, columns], result[:])
 
         products = [quantise_and_multiply(i) for i in range(chunks)]
-        waiting = scale(0)
-        for i in range(1, chunks):
-            scaled = scale(i)
-            shift_and_store(i - 1, waiting)
+        pieces = [(i, slice(0, CHUNK)) for i in range(chunks - 1)]
+        pieces.extend((chunks - 1, part) for part in spans([CHUNK // LAST_PARTS] * LAST_PARTS))
+        waiting = scale(*pieces[0])
+        for piece in pieces[1:]:
+            scaled = scale(*piece)
+            shift_and_store(*waiting)
             waiting = scaled
-        shift_and_store(chunks - 1, waiting)
+        shift_and_store(*waiting)

@@ -24,7 +24,8 @@ SCALE_ROWS = 4
 STRIPE = 16
 CLASS_STEP = 512
 CHUNK = 256
-LAST_PARTS = 2
+LAST = 128
+GPSIMD_SHIFT = 192
 GATHERS = {
     2: (("vector", 512), ("scalar", 512)),
     0: (("vector", 352), ("scalar", 672)),
@@ -149,23 +150,27 @@ def tile_picked_cbn_none_e_kernel(tc, xT, w1_words, w1_scales, gamma, beta, offs
             )
             return acc
 
-        def scale(i, part):
-            columns = slice(i * CHUNK + part.start, i * CHUNK + part.stop)
-            scaled = keep.tile([P, part.stop - part.start], F32, name=f"scaled{columns.start}")
-            nc.vector.tensor_tensor(scaled[:], products[i][:, part], gamma_picked[:, columns], MULT)
-            return columns, scaled
+        scaled = keep.tile([P, S], F32, name="scaled")
+        result = keep.tile([P, S], F32, name="result")
 
-        def shift_and_store(columns, scaled):
-            result = keep.tile([P, columns.stop - columns.start], F32, name=f"result{columns.start}")
-            nc.vector.tensor_tensor(result[:], scaled[:], beta_picked[:, columns], ADD)
-            nc.sync.dma_start(out[:, columns], result[:])
+        def scale(first, stop):
+            i = first // CHUNK
+            acc = products[i][:, first - i * CHUNK : stop - i * CHUNK]
+            nc.vector.tensor_tensor(scaled[:, first:stop], acc, gamma_picked[:, first:stop], MULT)
+
+        def shift_and_store(engine, first, stop):
+            engine.tensor_tensor(result[:, first:stop], scaled[:, first:stop], beta_picked[:, first:stop], ADD)
+            nc.sync.dma_start(out[:, first:stop], result[:, first:stop])
 
         products = [quantise_and_multiply(i) for i in range(chunks)]
-        pieces = [(i, slice(0, CHUNK)) for i in range(chunks - 1)]
-        pieces.extend((chunks - 1, part) for part in spans([CHUNK // LAST_PARTS] * LAST_PARTS))
-        waiting = scale(*pieces[0])
-        for piece in pieces[1:]:
-            scaled = scale(*piece)
-            shift_and_store(*waiting)
-            waiting = scaled
-        shift_and_store(*waiting)
+        scale(0, GPSIMD_SHIFT)
+        shift_and_store(nc.gpsimd, 0, GPSIMD_SHIFT)
+        scale(GPSIMD_SHIFT, CHUNK)
+        scale(CHUNK, 2 * CHUNK)
+        scale(2 * CHUNK, 3 * CHUNK)
+        shift_and_store(nc.vector, GPSIMD_SHIFT, 2 * CHUNK)
+        scale(3 * CHUNK, S - LAST)
+        shift_and_store(nc.vector, 2 * CHUNK, 3 * CHUNK)
+        scale(S - LAST, S)
+        shift_and_store(nc.vector, 3 * CHUNK, S - LAST)
+        shift_and_store(nc.vector, S - LAST, S)

@@ -22,34 +22,14 @@ PACK = 4
 QUADRANT = 32
 SCALE_ROWS = 4
 STRIPE = 16
-CLASS_STEP = 512
 CHUNK = 256
+DIRECT = (640, 256)
+FUSED = 256
 LAST = 128
-GPSIMD_SHIFT = 192
-GATHERS = {
-    2: (("vector", 512), ("scalar", 512)),
-    0: (("vector", 352), ("scalar", 672)),
-    1: (("vector", 352), ("scalar", 672)),
-    3: (("vector", 256), ("vector", 256), ("scalar", 256), ("scalar", 256)),
-}
-ROW_LOADS = {
-    2: ((("gpsimd", 960), ("scalar", 1088)),),
-    0: ((("vector", 1408),), (("gpsimd", 640),)),
-    1: ((("vector", 1408),), (("gpsimd", 640),)),
-    3: ((("gpsimd", 640),), (("gpsimd", 384), ("scalar", 512)), (("gpsimd", 320), ("scalar", 192))),
-}
 
 
-def spans(widths, start=0):
-    result = []
-    for width in widths:
-        result.append(slice(start, start + width))
-        start = start + width
-    return result
-
-
-def entries(list_tile, first, count):
-    return list_tile[:, first // STRIPE : (first + count) // STRIPE]
+def entries(list_tile, first, stop):
+    return list_tile[:, first // STRIPE : stop // STRIPE]
 
 
 def tile_picked_cbn_none_e_kernel(tc, xT, w1_words, w1_scales, gamma, beta, offs, cls, out):
@@ -66,68 +46,43 @@ def tile_picked_cbn_none_e_kernel(tc, xT, w1_words, w1_scales, gamma, beta, offs
         gamma_sb = keep.tile([P, U], F32, name="gamma_sb")
         beta_sb = keep.tile([P, U], F32, name="beta_sb")
         raw = [keep.tile([P, T], F32, name=f"raw{j}") for j in range(PACK)]
-        rounded = [keep.tile([P, T], BF16, name=f"rounded{j}") for j in range(PACK)]
         w_codes = keep.tile([P, 2 * N], U8, name="w_codes", align_bytes=64)
         w_scales = keep.tile([P, N], U8, name="w_scales", align_bytes=64)
         picked = keep.tile([P, S, PACK], BF16, name="picked", align_bytes=64)
+        planes = [keep.tile([P, 2, S], BF16, name=f"planes{u}") for u in range(2)]
+        gamma_picked = keep.tile([P, S], F32, name="gamma_picked")
+        beta_picked = keep.tile([P, S], F32, name="beta_picked")
+        scaled = keep.tile([P, S], F32, name="scaled")
+        result = keep.tile([P, S], F32, name="result")
 
         nc.gpsimd.memset(w_scales[:], 0)
 
-        def load_spans(j):
-            return spans([sum(width for engine, width in load) for load in ROW_LOADS[j]])
-
-        def load_row(j):
-            for c in load_spans(j):
-                nc.sync.dma_start(raw[j][:, c], x_rows[:, j, c])
-
-        nc.sync.dma_start(gamma_sb[:], gamma)
-        nc.sync.dma_start(cls_sb[:], cls)
+        nc.sync.dma_start(raw[0][:], x_rows[:, 0, :])
         nc.sync.dma_start(offs_sb[:], offs)
-        load_row(2)
-        load_row(0)
-        load_row(1)
-        nc.sync.dma_start(beta_sb[:], beta)
-        load_row(3)
+        for j in range(1, PACK):
+            nc.sync.dma_start(raw[j][:], x_rows[:, j, :])
         nc.sync.dma_start(w_codes[:].bitcast(I32), w1_words[0].bitcast(I32))
         for quad in range(P // QUADRANT):
             nc.sync.dma_start(
                 w_scales[QUADRANT * quad : QUADRANT * quad + SCALE_ROWS, :].bitcast(I32),
                 w1_scales[0, SCALE_ROWS * quad : SCALE_ROWS * (quad + 1), :].bitcast(I32),
             )
+        nc.sync.dma_start(cls_sb[:], cls)
+        nc.sync.dma_start(gamma_sb[:], gamma)
+        nc.sync.dma_start(beta_sb[:], beta)
 
-        def gather_by_class(table, name):
-            looked_up = keep.tile([P, S], F32, name=name)
-            for first in range(0, S, CLASS_STEP):
-                nc.vector.tensor_copy(
-                    looked_up[:, first : first + CLASS_STEP], table[:].indirect(entries(cls_sb, first, CLASS_STEP))
-                )
-            return looked_up
+        def gather_direct(j):
+            nc.vector.tensor_copy(picked[:, 0 : DIRECT[j // 2], j], raw[j][:].indirect(entries(offs_sb, 0, DIRECT[j // 2])))
 
-        def round_row(j):
-            for load, load_span in zip(ROW_LOADS[j], load_spans(j)):
-                for (engine, width), c in zip(load, spans([width for engine, width in load], load_span.start)):
-                    if engine == "gpsimd":
-                        nc.gpsimd.tensor_scalar(rounded[j][:, c], raw[j][:, c], 1.0, 0.0, MULT, ADD)
-                    elif engine == "scalar":
-                        nc.scalar.activation(rounded[j][:, c], raw[j][:, c], COPY)
-                    else:
-                        nc.vector.tensor_copy(rounded[j][:, c], raw[j][:, c])
+        def gather_plane(j, first, stop):
+            nc.scalar.activation(
+                planes[j // 2][:, j % 2, first:stop], raw[j][:].indirect(entries(offs_sb, first, stop)), COPY
+            )
 
-        def gather_row(j):
-            for (engine, count), c in zip(GATHERS[j], spans([count for engine, count in GATHERS[j]])):
-                offsets = entries(offs_sb, c.start, count)
-                if engine == "vector":
-                    nc.vector.tensor_copy(picked[:, c, j], raw[j][:].indirect(offsets))
-                else:
-                    nc.scalar.activation(picked[:, c, j], rounded[j][:].indirect(offsets), COPY)
-
-        gamma_picked = gather_by_class(gamma_sb, "gamma_picked")
-        for j in (2, 0, 1):
-            round_row(j)
-            gather_row(j)
-        beta_picked = gather_by_class(beta_sb, "beta_picked")
-        round_row(3)
-        gather_row(3)
+        def place_pair(u, first, stop):
+            nc.vector.tensor_copy(
+                picked[:, first:stop, 2 * u : 2 * u + 2], planes[u][:, :, first:stop].rearrange("p t s -> p s t")
+            )
 
         def quantise_and_multiply(i):
             columns = slice(i * CHUNK, (i + 1) * CHUNK)
@@ -150,27 +105,45 @@ def tile_picked_cbn_none_e_kernel(tc, xT, w1_words, w1_scales, gamma, beta, offs
             )
             return acc
 
-        scaled = keep.tile([P, S], F32, name="scaled")
-        result = keep.tile([P, S], F32, name="result")
+        for j in range(PACK - 1):
+            gather_direct(j)
+            gather_plane(j, DIRECT[j // 2], S)
+            if j == 1:
+                place_pair(0, DIRECT[0], S)
 
-        def scale(first, stop):
-            i = first // CHUNK
-            acc = products[i][:, first - i * CHUNK : stop - i * CHUNK]
-            nc.vector.tensor_tensor(scaled[:, first:stop], acc, gamma_picked[:, first:stop], MULT)
+        gather_direct(PACK - 1)
+        products = []
+        for i in range(chunks):
+            if i + 1 < chunks:
+                gather_plane(PACK - 1, (i + 1) * CHUNK, (i + 2) * CHUNK)
+                place_pair(1, (i + 1) * CHUNK, (i + 2) * CHUNK)
+            products.append(quantise_and_multiply(i))
 
-        def shift_and_store(engine, first, stop):
-            engine.tensor_tensor(result[:, first:stop], scaled[:, first:stop], beta_picked[:, first:stop], ADD)
+        def look_up(looked_up, table, first, stop):
+            nc.scalar.activation(looked_up[:, first:stop], table[:].indirect(entries(cls_sb, first, stop)), COPY)
+
+        def scale(i):
+            columns = slice(i * CHUNK, (i + 1) * CHUNK)
+            nc.vector.tensor_tensor(scaled[:, columns], products[i][:], gamma_picked[:, columns], MULT)
+
+        def shift_and_store(first, stop):
+            if stop <= FUSED:
+                shift = beta_sb[:].indirect(entries(cls_sb, first, stop))
+            else:
+                shift = beta_picked[:, first:stop]
+            nc.vector.tensor_tensor(result[:, first:stop], shift, scaled[:, first:stop], ADD)
             nc.sync.dma_start(out[:, first:stop], result[:, first:stop])
 
-        products = [quantise_and_multiply(i) for i in range(chunks)]
-        scale(0, GPSIMD_SHIFT)
-        shift_and_store(nc.gpsimd, 0, GPSIMD_SHIFT)
-        scale(GPSIMD_SHIFT, CHUNK)
-        scale(CHUNK, 2 * CHUNK)
-        scale(2 * CHUNK, 3 * CHUNK)
-        shift_and_store(nc.vector, GPSIMD_SHIFT, 2 * CHUNK)
-        scale(3 * CHUNK, S - LAST)
-        shift_and_store(nc.vector, 2 * CHUNK, 3 * CHUNK)
-        scale(S - LAST, S)
-        shift_and_store(nc.vector, 3 * CHUNK, S - LAST)
-        shift_and_store(nc.vector, S - LAST, S)
+        for i in range(chunks):
+            look_up(gamma_picked, gamma_sb, i * CHUNK, (i + 1) * CHUNK)
+        pieces = [(CHUNK, 2 * CHUNK), (2 * CHUNK, 3 * CHUNK), (3 * CHUNK, S - LAST), (S - LAST, S)]
+        for first, stop in pieces:
+            look_up(beta_picked, beta_sb, first, stop)
+
+        scale(0)
+        scale(1)
+        shift_and_store(0, FUSED)
+        scale(2)
+        scale(3)
+        for first, stop in pieces:
+            shift_and_store(first, stop)

@@ -24,7 +24,8 @@ SCALE_ROWS = 4
 STRIPE = 16
 CHUNK = 256
 DIRECT = (640, 256)
-FUSED = 256
+FUSED = 384
+CLASS_STEP = 512
 LAST = 128
 
 
@@ -57,16 +58,21 @@ def tile_picked_cbn_none_e_kernel(tc, xT, w1_words, w1_scales, gamma, beta, offs
 
         nc.gpsimd.memset(w_scales[:], 0)
 
-        nc.sync.dma_start(raw[0][:], x_rows[:, 0, :])
-        nc.sync.dma_start(offs_sb[:], offs)
-        for j in range(1, PACK):
-            nc.sync.dma_start(raw[j][:], x_rows[:, j, :])
-        nc.sync.dma_start(w_codes[:].bitcast(I32), w1_words[0].bitcast(I32))
-        for quad in range(P // QUADRANT):
+        def load_scale_rows(quad):
             nc.sync.dma_start(
                 w_scales[QUADRANT * quad : QUADRANT * quad + SCALE_ROWS, :].bitcast(I32),
                 w1_scales[0, SCALE_ROWS * quad : SCALE_ROWS * (quad + 1), :].bitcast(I32),
             )
+
+        nc.sync.dma_start(raw[0][:], x_rows[:, 0, :])
+        nc.sync.dma_start(offs_sb[:], offs)
+        nc.sync.dma_start(raw[1][:], x_rows[:, 1, :])
+        nc.sync.dma_start(raw[2][:], x_rows[:, 2, :])
+        load_scale_rows(0)
+        nc.sync.dma_start(raw[3][:], x_rows[:, 3, :])
+        nc.sync.dma_start(w_codes[:].bitcast(I32), w1_words[0].bitcast(I32))
+        for quad in range(1, P // QUADRANT):
+            load_scale_rows(quad)
         nc.sync.dma_start(cls_sb[:], cls)
         nc.sync.dma_start(gamma_sb[:], gamma)
         nc.sync.dma_start(beta_sb[:], beta)
@@ -126,24 +132,28 @@ def tile_picked_cbn_none_e_kernel(tc, xT, w1_words, w1_scales, gamma, beta, offs
             columns = slice(i * CHUNK, (i + 1) * CHUNK)
             nc.vector.tensor_tensor(scaled[:, columns], products[i][:], gamma_picked[:, columns], MULT)
 
-        def shift_and_store(first, stop):
-            if stop <= FUSED:
-                shift = beta_sb[:].indirect(entries(cls_sb, first, stop))
-            else:
-                shift = beta_picked[:, first:stop]
-            nc.vector.tensor_tensor(result[:, first:stop], shift, scaled[:, first:stop], ADD)
-            nc.sync.dma_start(out[:, first:stop], result[:, first:stop])
+        def shift_and_store(shifted, shift, first, stop):
+            nc.vector.tensor_tensor(shifted, shift, scaled[:, first:stop], ADD)
+            nc.sync.dma_start(out[:, first:stop], shifted)
 
-        for i in range(chunks):
-            look_up(gamma_picked, gamma_sb, i * CHUNK, (i + 1) * CHUNK)
-        pieces = [(CHUNK, 2 * CHUNK), (2 * CHUNK, 3 * CHUNK), (3 * CHUNK, S - LAST), (S - LAST, S)]
+        def shift_looked_up(first, stop):
+            shift_and_store(result[:, first:stop], beta_picked[:, first:stop], first, stop)
+
+        def shift_fused(shifted, first, stop):
+            shift_and_store(shifted, beta_sb[:].indirect(entries(cls_sb, first, stop)), first, stop)
+
+        for first in range(0, S, CLASS_STEP):
+            look_up(gamma_picked, gamma_sb, first, first + CLASS_STEP)
+        pieces = [(FUSED, FUSED + CHUNK), (FUSED + CHUNK, S - LAST), (S - LAST, S)]
         for first, stop in pieces:
             look_up(beta_picked, beta_sb, first, stop)
 
         scale(0)
         scale(1)
-        shift_and_store(0, FUSED)
+        shift_fused(result[:, 0:CHUNK], 0, CHUNK)
         scale(2)
         scale(3)
-        for first, stop in pieces:
-            shift_and_store(first, stop)
+        shift_looked_up(*pieces[0])
+        shift_fused(gamma_picked[:, 2 * CHUNK : CHUNK + FUSED], CHUNK, FUSED)
+        shift_looked_up(*pieces[1])
+        shift_looked_up(*pieces[2])

@@ -26,6 +26,7 @@ CHUNK = 256
 DIRECT = (640, 256)
 FUSED = 384
 CLASS_STEP = 512
+DMA_ALIGN = 256
 LAST = 128
 
 
@@ -42,19 +43,19 @@ def tile_picked_cbn_none_e_kernel(tc, xT, w1_words, w1_scales, gamma, beta, offs
         keep = ctx.enter_context(tc.tile_pool(name="keep", bufs=1))
         psum = ctx.enter_context(tc.psum_pool(name="psum", bufs=1))
 
-        offs_sb = keep.tile([P, S // STRIPE], U16, name="offs_sb")
+        offs_sb = keep.tile([P, S // STRIPE], U16, name="offs_sb", align_bytes=DMA_ALIGN)
         cls_sb = keep.tile([P, S // STRIPE], U16, name="cls_sb")
-        gamma_sb = keep.tile([P, U], F32, name="gamma_sb")
-        beta_sb = keep.tile([P, U], F32, name="beta_sb")
-        raw = [keep.tile([P, T], F32, name=f"raw{j}") for j in range(PACK)]
+        gamma_sb = keep.tile([P, U], F32, name="gamma_sb", align_bytes=DMA_ALIGN)
+        beta_sb = keep.tile([P, U], F32, name="beta_sb", align_bytes=DMA_ALIGN)
+        raw = [keep.tile([P, T], F32, name=f"raw{j}", align_bytes=DMA_ALIGN) for j in range(PACK)]
         w_codes = keep.tile([P, 2 * N], U8, name="w_codes", align_bytes=64)
         w_scales = keep.tile([P, N], U8, name="w_scales", align_bytes=64)
         picked = keep.tile([P, S, PACK], BF16, name="picked", align_bytes=64)
         planes = [keep.tile([P, 2, S], BF16, name=f"planes{u}") for u in range(2)]
-        gamma_picked = keep.tile([P, S], F32, name="gamma_picked")
+        gamma_picked = keep.tile([P, S], F32, name="gamma_picked", align_bytes=DMA_ALIGN)
         beta_picked = keep.tile([P, S], F32, name="beta_picked")
         scaled = keep.tile([P, S], F32, name="scaled")
-        result = keep.tile([P, S], F32, name="result")
+        result = keep.tile([P, S], F32, name="result", align_bytes=DMA_ALIGN)
 
         nc.gpsimd.memset(w_scales[:], 0)
 

@@ -59,21 +59,22 @@ def tile_picked_cbn_none_e_kernel(tc, xT, w1_words, w1_scales, gamma, beta, offs
 
         nc.gpsimd.memset(w_scales[:], 0)
 
-        def load_scale_rows(quad):
-            nc.sync.dma_start(
+        def load_scale_rows(queue, quad):
+            queue.dma_start(
                 w_scales[QUADRANT * quad : QUADRANT * quad + SCALE_ROWS, :].bitcast(I32),
                 w1_scales[0, SCALE_ROWS * quad : SCALE_ROWS * (quad + 1), :].bitcast(I32),
             )
 
+        load_scale_rows(nc.gpsimd, 0)
+        load_scale_rows(nc.gpsimd, 1)
         nc.sync.dma_start(raw[0][:], x_rows[:, 0, :])
         nc.sync.dma_start(offs_sb[:], offs)
         nc.sync.dma_start(raw[1][:], x_rows[:, 1, :])
         nc.sync.dma_start(raw[2][:], x_rows[:, 2, :])
-        load_scale_rows(0)
         nc.sync.dma_start(raw[3][:], x_rows[:, 3, :])
         nc.sync.dma_start(w_codes[:].bitcast(I32), w1_words[0].bitcast(I32))
-        for quad in range(1, P // QUADRANT):
-            load_scale_rows(quad)
+        load_scale_rows(nc.sync, 2)
+        load_scale_rows(nc.sync, 3)
         nc.sync.dma_start(cls_sb[:], cls)
         nc.sync.dma_start(gamma_sb[:], gamma)
         nc.sync.dma_start(beta_sb[:], beta)

@@ -22,11 +22,13 @@ PACK = 4
 QUADRANT = 32
 SCALE_ROWS = 4
 STRIPE = 16
-CHUNK = 256
-DIRECT = (640, 256)
-FUSED = 384
-CLASS_STEP = 512
+MX_ALIGN = 64
 DMA_ALIGN = 256
+CHUNK = 256
+DIRECT = (640, CHUNK)
+CLASS_STEP = 512
+SCALINGS = ((0, CHUNK), (CHUNK, 2 * CHUNK), (2 * CHUNK, S))
+FUSED_LATE = 128
 LAST = 128
 
 
@@ -37,6 +39,7 @@ def entries(list_tile, first, stop):
 def tile_picked_cbn_none_e_kernel(tc, xT, w1_words, w1_scales, gamma, beta, offs, cls, out):
     nc = tc.nc
     chunks = S // CHUNK
+    last_row = PACK - 1
     x_rows = xT.rearrange("(p j) t -> p j t", j=PACK)
 
     with ExitStack() as ctx:
@@ -48,10 +51,10 @@ def tile_picked_cbn_none_e_kernel(tc, xT, w1_words, w1_scales, gamma, beta, offs
         gamma_sb = keep.tile([P, U], F32, name="gamma_sb", align_bytes=DMA_ALIGN)
         beta_sb = keep.tile([P, U], F32, name="beta_sb", align_bytes=DMA_ALIGN)
         raw = [keep.tile([P, T], F32, name=f"raw{j}", align_bytes=DMA_ALIGN) for j in range(PACK)]
-        w_codes = keep.tile([P, 2 * N], U8, name="w_codes", align_bytes=64)
-        w_scales = keep.tile([P, N], U8, name="w_scales", align_bytes=64)
-        picked = keep.tile([P, S, PACK], BF16, name="picked", align_bytes=64)
-        planes = [keep.tile([P, 2, S], BF16, name=f"planes{u}") for u in range(2)]
+        w_codes = keep.tile([P, 2 * N], U8, name="w_codes", align_bytes=MX_ALIGN)
+        w_scales = keep.tile([P, N], U8, name="w_scales", align_bytes=MX_ALIGN)
+        picked = keep.tile([P, S, PACK], BF16, name="picked", align_bytes=MX_ALIGN)
+        planes = [keep.tile([P, 2, S], BF16, name=f"planes{u}") for u in range(PACK // 2)]
         gamma_picked = keep.tile([P, S], F32, name="gamma_picked", align_bytes=DMA_ALIGN)
         beta_picked = keep.tile([P, S], F32, name="beta_picked")
         scaled = keep.tile([P, S], F32, name="scaled")
@@ -69,9 +72,8 @@ def tile_picked_cbn_none_e_kernel(tc, xT, w1_words, w1_scales, gamma, beta, offs
         load_scale_rows(nc.gpsimd, 1)
         nc.sync.dma_start(raw[0][:], x_rows[:, 0, :])
         nc.sync.dma_start(offs_sb[:], offs)
-        nc.sync.dma_start(raw[1][:], x_rows[:, 1, :])
-        nc.sync.dma_start(raw[2][:], x_rows[:, 2, :])
-        nc.sync.dma_start(raw[3][:], x_rows[:, 3, :])
+        for j in range(1, PACK):
+            nc.sync.dma_start(raw[j][:], x_rows[:, j, :])
         nc.sync.dma_start(w_codes[:].bitcast(I32), w1_words[0].bitcast(I32))
         load_scale_rows(nc.sync, 2)
         load_scale_rows(nc.sync, 3)
@@ -80,7 +82,8 @@ def tile_picked_cbn_none_e_kernel(tc, xT, w1_words, w1_scales, gamma, beta, offs
         nc.sync.dma_start(beta_sb[:], beta)
 
         def gather_direct(j):
-            nc.vector.tensor_copy(picked[:, 0 : DIRECT[j // 2], j], raw[j][:].indirect(entries(offs_sb, 0, DIRECT[j // 2])))
+            count = DIRECT[j // 2]
+            nc.vector.tensor_copy(picked[:, 0:count, j], raw[j][:].indirect(entries(offs_sb, 0, count)))
 
         def gather_plane(j, first, stop):
             nc.scalar.activation(
@@ -92,18 +95,24 @@ def tile_picked_cbn_none_e_kernel(tc, xT, w1_words, w1_scales, gamma, beta, offs
                 picked[:, first:stop, 2 * u : 2 * u + 2], planes[u][:, :, first:stop].rearrange("p t s -> p s t")
             )
 
+        banks = [psum.tile([P, stop - first], F32, name=f"bank{first}") for first, stop in SCALINGS]
+
+        def product(first, stop):
+            for (bank_first, bank_stop), bank in zip(SCALINGS, banks):
+                if bank_first <= first < bank_stop:
+                    return bank[:, first - bank_first : stop - bank_first]
+
         def quantise_and_multiply(i):
-            columns = slice(i * CHUNK, (i + 1) * CHUNK)
-            codes = keep.tile([P, CHUNK], U32, name=f"codes{i}", align_bytes=64)
-            scales = keep.tile([P, CHUNK], U8, name=f"scales{i}", align_bytes=64)
+            first, stop = i * CHUNK, (i + 1) * CHUNK
+            codes = keep.tile([P, CHUNK], U32, name=f"codes{i}", align_bytes=MX_ALIGN)
+            scales = keep.tile([P, CHUNK], U8, name=f"scales{i}", align_bytes=MX_ALIGN)
             nc.vector.quantize_mx(
                 out=codes[:].bitcast(FP8X4),
                 scales=scales[:],
-                in_=picked[:, columns, :].rearrange("p s j -> p (s j)"),
+                in_=picked[:, first:stop, :].rearrange("p s j -> p (s j)"),
             )
-            acc = psum.tile([P, CHUNK], F32, name=f"acc{i}")
             nc.tensor.matmul_mx(
-                out=acc[:],
+                out=product(first, stop),
                 lhsT=w_codes[:].bitcast(FP4X4),
                 lhsT_scale=w_scales[:],
                 rhs=codes[:].bitcast(FP8X4),
@@ -111,51 +120,49 @@ def tile_picked_cbn_none_e_kernel(tc, xT, w1_words, w1_scales, gamma, beta, offs
                 start=True,
                 stop=True,
             )
-            return acc
 
-        for j in range(PACK - 1):
+        for j in range(last_row):
             gather_direct(j)
             gather_plane(j, DIRECT[j // 2], S)
             if j == 1:
                 place_pair(0, DIRECT[0], S)
 
-        gather_direct(PACK - 1)
-        products = []
+        gather_direct(last_row)
         for i in range(chunks):
             if i + 1 < chunks:
-                gather_plane(PACK - 1, (i + 1) * CHUNK, (i + 2) * CHUNK)
-                place_pair(1, (i + 1) * CHUNK, (i + 2) * CHUNK)
-            products.append(quantise_and_multiply(i))
+                gather_plane(last_row, (i + 1) * CHUNK, (i + 2) * CHUNK)
+                place_pair(last_row // 2, (i + 1) * CHUNK, (i + 2) * CHUNK)
+            quantise_and_multiply(i)
 
         def look_up(looked_up, table, first, stop):
             nc.scalar.activation(looked_up[:, first:stop], table[:].indirect(entries(cls_sb, first, stop)), COPY)
 
         def scale(i):
-            columns = slice(i * CHUNK, (i + 1) * CHUNK)
-            nc.vector.tensor_tensor(scaled[:, columns], products[i][:], gamma_picked[:, columns], MULT)
+            first, stop = SCALINGS[i]
+            nc.vector.tensor_tensor(scaled[:, first:stop], banks[i][:], gamma_picked[:, first:stop], MULT)
 
-        def shift_and_store(shifted, shift, first, stop):
-            nc.vector.tensor_tensor(shifted, shift, scaled[:, first:stop], ADD)
-            nc.sync.dma_start(out[:, first:stop], shifted)
+        def shift_and_store(shift, first, stop):
+            nc.vector.tensor_tensor(result[:, first:stop], shift, scaled[:, first:stop], ADD)
+            nc.sync.dma_start(out[:, first:stop], result[:, first:stop])
 
         def shift_looked_up(first, stop):
-            shift_and_store(result[:, first:stop], beta_picked[:, first:stop], first, stop)
+            shift_and_store(beta_picked[:, first:stop], first, stop)
 
-        def shift_fused(shifted, first, stop):
-            shift_and_store(shifted, beta_sb[:].indirect(entries(cls_sb, first, stop)), first, stop)
+        def shift_fused(first, stop):
+            shift_and_store(beta_sb[:].indirect(entries(cls_sb, first, stop)), first, stop)
 
+        fused_stop = 2 * CHUNK + FUSED_LATE
+        beta_spans = [(CHUNK, 2 * CHUNK), (fused_stop, S - LAST), (S - LAST, S)]
         for first in range(0, S, CLASS_STEP):
             look_up(gamma_picked, gamma_sb, first, first + CLASS_STEP)
-        pieces = [(FUSED, FUSED + CHUNK), (FUSED + CHUNK, S - LAST), (S - LAST, S)]
-        for first, stop in pieces:
+        for first, stop in beta_spans:
             look_up(beta_picked, beta_sb, first, stop)
 
         scale(0)
         scale(1)
-        shift_fused(result[:, 0:CHUNK], 0, CHUNK)
+        shift_fused(0, CHUNK)
         scale(2)
-        scale(3)
-        shift_looked_up(*pieces[0])
-        shift_fused(gamma_picked[:, 2 * CHUNK : CHUNK + FUSED], CHUNK, FUSED)
-        shift_looked_up(*pieces[1])
-        shift_looked_up(*pieces[2])
+        shift_looked_up(*beta_spans[0])
+        shift_fused(2 * CHUNK, fused_stop)
+        shift_looked_up(*beta_spans[1])
+        shift_looked_up(*beta_spans[2])

@@ -28,7 +28,7 @@ CHUNK = 256
 DIRECT = (640, CHUNK)
 CLASS_STEP = 512
 SCALINGS = ((0, CHUNK), (CHUNK, 2 * CHUNK), (2 * CHUNK, S))
-FUSED_LATE = 128
+FUSED_LATE = 192
 LAST = 128
 
 

from contextlib import ExitStack

import concourse.mybir as mybir

K, T, S, N, U = 512, 2048, 1024, 128, 1024
FLOPS = 2 * K * S * N + 2 * S * N

F32 = mybir.dt.float32
BF16 = mybir.dt.bfloat16
I32 = mybir.dt.int32
U32 = mybir.dt.uint32
U16 = mybir.dt.uint16
U8 = mybir.dt.uint8
FP8X4 = mybir.dt.float8_e4m3fn_x4
FP4X4 = mybir.dt.float4_e2m1fn_x4
COPY = mybir.ActivationFunctionType.Copy
MULT = mybir.AluOpType.mult
ADD = mybir.AluOpType.add

P = 128
PACK = 4
QUADRANT = 32
SCALE_ROWS = 4
STRIPE = 16
MX_ALIGN = 64
DMA_ALIGN = 256
CHUNK = 256
DIRECT = (640, CHUNK)
CLASS_STEP = 512
SCALINGS = ((0, CHUNK), (CHUNK, 2 * CHUNK), (2 * CHUNK, S))
FUSED_LATE = 192
LAST = 128


def entries(list_tile, first, stop):
    return list_tile[:, first // STRIPE : stop // STRIPE]


def tile_picked_cbn_none_e_kernel(tc, xT, w1_words, w1_scales, gamma, beta, offs, cls, out):
    nc = tc.nc
    chunks = S // CHUNK
    last_row = PACK - 1
    x_rows = xT.rearrange("(p j) t -> p j t", j=PACK)

    with ExitStack() as ctx:
        keep = ctx.enter_context(tc.tile_pool(name="keep", bufs=1))
        psum = ctx.enter_context(tc.psum_pool(name="psum", bufs=1))

        offs_sb = keep.tile([P, S // STRIPE], U16, name="offs_sb", align_bytes=DMA_ALIGN)
        cls_sb = keep.tile([P, S // STRIPE], U16, name="cls_sb")
        gamma_sb = keep.tile([P, U], F32, name="gamma_sb", align_bytes=DMA_ALIGN)
        beta_sb = keep.tile([P, U], F32, name="beta_sb", align_bytes=DMA_ALIGN)
        raw = [keep.tile([P, T], F32, name=f"raw{j}", align_bytes=DMA_ALIGN) for j in range(PACK)]
        w_codes = keep.tile([P, 2 * N], U8, name="w_codes", align_bytes=MX_ALIGN)
        w_scales = keep.tile([P, N], U8, name="w_scales", align_bytes=MX_ALIGN)
        picked = keep.tile([P, S, PACK], BF16, name="picked", align_bytes=MX_ALIGN)
        planes = [keep.tile([P, 2, S], BF16, name=f"planes{u}") for u in range(PACK // 2)]
        gamma_picked = keep.tile([P, S], F32, name="gamma_picked", align_bytes=DMA_ALIGN)
        beta_picked = keep.tile([P, S], F32, name="beta_picked")
        scaled = keep.tile([P, S], F32, name="scaled")
        result = keep.tile([P, S], F32, name="result", align_bytes=DMA_ALIGN)

        nc.gpsimd.memset(w_scales[:], 0)

        def load_scale_rows(queue, quad):
            queue.dma_start(
                w_scales[QUADRANT * quad : QUADRANT * quad + SCALE_ROWS, :].bitcast(I32),
                w1_scales[0, SCALE_ROWS * quad : SCALE_ROWS * (quad + 1), :].bitcast(I32),
            )

        load_scale_rows(nc.gpsimd, 0)
        load_scale_rows(nc.gpsimd, 1)
        nc.sync.dma_start(raw[0][:], x_rows[:, 0, :])
        nc.sync.dma_start(offs_sb[:], offs)
        for j in range(1, PACK):
            nc.sync.dma_start(raw[j][:], x_rows[:, j, :])
        nc.sync.dma_start(w_codes[:].bitcast(I32), w1_words[0].bitcast(I32))
        load_scale_rows(nc.sync, 2)
        load_scale_rows(nc.sync, 3)
        nc.sync.dma_start(cls_sb[:], cls)
        nc.sync.dma_start(gamma_sb[:], gamma)
        nc.sync.dma_start(beta_sb[:], beta)

        def gather_direct(j):
            count = DIRECT[j // 2]
            nc.vector.tensor_copy(picked[:, 0:count, j], raw[j][:].indirect(entries(offs_sb, 0, count)))

        def gather_plane(j, first, stop):
            nc.scalar.activation(
                planes[j // 2][:, j % 2, first:stop], raw[j][:].indirect(entries(offs_sb, first, stop)), COPY
            )

        def place_pair(u, first, stop):
            nc.vector.tensor_copy(
                picked[:, first:stop, 2 * u : 2 * u + 2], planes[u][:, :, first:stop].rearrange("p t s -> p s t")
            )

        banks = [psum.tile([P, stop - first], F32, name=f"bank{first}") for first, stop in SCALINGS]

        def product(first, stop):
            for (bank_first, bank_stop), bank in zip(SCALINGS, banks):
                if bank_first <= first < bank_stop:
                    return bank[:, first - bank_first : stop - bank_first]

        def quantise_and_multiply(i):
            first, stop = i * CHUNK, (i + 1) * CHUNK
            codes = keep.tile([P, CHUNK], U32, name=f"codes{i}", align_bytes=MX_ALIGN)
            scales = keep.tile([P, CHUNK], U8, name=f"scales{i}", align_bytes=MX_ALIGN)
            nc.vector.quantize_mx(
                out=codes[:].bitcast(FP8X4),
                scales=scales[:],
                in_=picked[:, first:stop, :].rearrange("p s j -> p (s j)"),
            )
            nc.tensor.matmul_mx(
                out=product(first, stop),
                lhsT=w_codes[:].bitcast(FP4X4),
                lhsT_scale=w_scales[:],
                rhs=codes[:].bitcast(FP8X4),
                rhs_scale=scales[:],
                start=True,
                stop=True,
            )

        for j in range(last_row):
            gather_direct(j)
            gather_plane(j, DIRECT[j // 2], S)
            if j == 1:
                place_pair(0, DIRECT[0], S)

        gather_direct(last_row)
        for i in range(chunks):
            if i + 1 < chunks:
                gather_plane(last_row, (i + 1) * CHUNK, (i + 2) * CHUNK)
                place_pair(last_row // 2, (i + 1) * CHUNK, (i + 2) * CHUNK)
            quantise_and_multiply(i)

        def look_up(looked_up, table, first, stop):
            nc.scalar.activation(looked_up[:, first:stop], table[:].indirect(entries(cls_sb, first, stop)), COPY)

        def scale(i):
            first, stop = SCALINGS[i]
            nc.vector.tensor_tensor(scaled[:, first:stop], banks[i][:], gamma_picked[:, first:stop], MULT)

        def shift_and_store(shift, first, stop):
            nc.vector.tensor_tensor(result[:, first:stop], shift, scaled[:, first:stop], ADD)
            nc.sync.dma_start(out[:, first:stop], result[:, first:stop])

        def shift_looked_up(first, stop):
            shift_and_store(beta_picked[:, first:stop], first, stop)

        def shift_fused(first, stop):
            shift_and_store(beta_sb[:].indirect(entries(cls_sb, first, stop)), first, stop)

        fused_stop = 2 * CHUNK + FUSED_LATE
        beta_spans = [(CHUNK, 2 * CHUNK), (fused_stop, S - LAST), (S - LAST, S)]
        for first in range(0, S, CLASS_STEP):
            look_up(gamma_picked, gamma_sb, first, first + CLASS_STEP)
        for first, stop in beta_spans:
            look_up(beta_picked, beta_sb, first, stop)

        scale(0)
        scale(1)
        shift_fused(0, CHUNK)
        scale(2)
        shift_looked_up(*beta_spans[0])
        shift_fused(2 * CHUNK, fused_stop)
        shift_looked_up(*beta_spans[1])
        shift_looked_up(*beta_spans[2])
